import numpy as np
import ml_dtypes


def mxq(x, axis, fmt="e4m3"):
    dtype, down = {"e4m3": (ml_dtypes.float8_e4m3fn, 7), "e5m2": (ml_dtypes.float8_e5m2, 14)}[fmt]
    v = np.moveaxis(np.asarray(x, np.float32).astype(ml_dtypes.bfloat16).astype(np.float64), axis, -1)
    blocks = v.reshape(v.shape[:-1] + (-1, 32))
    amax = np.abs(blocks).max(-1, keepdims=True)
    byte = np.maximum(np.where(amax > 0, np.frexp(amax)[1] - 1 + 127, 0) - down, 1)
    scale = np.exp2(byte - 127.0)
    codes = (blocks / scale).astype(np.float32).astype(dtype).astype(np.float64)
    return np.moveaxis((codes * scale).reshape(v.shape), -1, axis)


WIDE = False


def mx_kscale(k):
    if not WIDE:
        return np.ones(k)
    levels = np.array([10, -10, 5, -5, 0])
    if k % 512:
        return np.exp2(np.random.permutation(np.resize(levels, k // 32))).repeat(32)
    a = np.empty((k // 512, 16))
    for p in range(k // 512):
        a[p, :8] = np.random.permutation(np.resize(levels, 8))
        for g in range(8):
            far = levels[np.abs(levels - a[p, g]) >= 10]
            a[p, g + 8] = far[np.random.randint(len(far))]
    return np.exp2(a.ravel()).repeat(32)


def f64(x):
    return np.asarray(x).astype(np.float64)


def striped(idx):
    return np.tile(idx.reshape(-1, 16).T, (8, 1)).astype(np.uint16)


def unstriped(offs):
    return offs[:16].T.reshape(-1).astype(np.int64)


def pack_weight(w):
    k, n = w.shape
    w = f64(np.asarray(w, np.float32).astype(ml_dtypes.bfloat16)).reshape(k // 32, 32, n)
    amax = np.abs(w).max(1)
    byte = np.clip(np.where(amax > 0, np.frexp(amax)[1] - 1 + 127 - 7, 1), 1, 254)
    scaled = (w * np.exp2(127.0 - byte)[:, None, :]).reshape(k, n).astype(np.float32)
    words = np.ascontiguousarray(scaled.reshape(k // 512, 128, 4, n).transpose(0, 1, 3, 2)).astype(ml_dtypes.float8_e4m3fn).view(np.uint8)
    return words, np.ascontiguousarray(byte.astype(np.uint8).reshape(k // 512, 16, n))


def unpack_weight(words, scales):
    g, p, n, _ = words.shape
    vals = np.ascontiguousarray(words).view(ml_dtypes.float8_e4m3fn).astype(np.float64) * np.repeat(np.exp2(scales.astype(np.float64) - 127.0), 8, axis=1)[..., None]
    return vals.transpose(0, 1, 3, 2).reshape(g * 512, n)


K, T, S, D, V, N = 512, 1024, 512, 4, 256, 128
P = 2 ** 7


def setup_inputs():
    n = np.random.standard_normal
    s = mx_kscale(K)[:, None]
    packed_w1 = pack_weight(n((K, N)) / np.sqrt(K) / s)
    return {
        "xT": (n((K, T)) * s).astype(np.float32),
        "w1_words": packed_w1[0],
        "w1_scales": packed_w1[1],
        "score": np.tile(np.random.standard_normal((D, 1, V)), (1, P, 1)).astype(np.float32),
        "offs": striped(np.random.permutation(T)[:S]),
        "pos1": striped(np.random.permutation(S)[:V]),
        "pos2": striped(np.random.permutation(S)[:V]),
        "pos3": striped(np.random.permutation(S)[:V]),
        "pos4": striped(np.random.permutation(S)[:V]),
    }


def reference(xT, w1_words, w1_scales, score, offs, pos1, pos2, pos3, pos4):
    xq = mxq(f64(xT)[:, unstriped(offs)], 0, "e4m3")
    y = unpack_weight(w1_words, w1_scales).T @ xq
    e0 = np.exp(f64(score)[0, :1])
    e1 = np.exp(f64(score)[1, :1])
    e2 = np.exp(f64(score)[2, :1])
    e3 = np.exp(f64(score)[3, :1])
    num = y[:, unstriped(pos1)] * e0 + y[:, unstriped(pos2)] * e1 + y[:, unstriped(pos3)] * e2 + y[:, unstriped(pos4)] * e3
    den = e0 + e1 + e2 + e3
    return num / den

@@ -1,0 +1,142 @@
+from contextlib import ExitStack
+
+import concourse.mybir as mybir
+from concourse.masks import make_identity
+
+F32 = mybir.dt.float32
+BF16 = mybir.dt.bfloat16
+I32 = mybir.dt.int32
+U32 = mybir.dt.uint32
+U16 = mybir.dt.uint16
+U8 = mybir.dt.uint8
+FP8X4 = mybir.dt.float8_e4m3fn_x4
+ALU = mybir.AluOpType
+ACT = mybir.ActivationFunctionType
+
+P = 128
+K, T, S, D, V, N = 512, 1024, 512, 4, 256, 128
+PACK = 4
+HALF = S // 2
+ROW_STEP = 7
+D_STEP = 38
+
+FLOPS = 2 * K * S * N
+BYTES = 4 * K * T + K * N + K * N // 32 + 4 * D * V + 2 * (S + D * V) + 4 * N * V
+
+
+def tile_picked_gatv_none_e_kernel(tc, xT, w1_words, w1_scales, score, offs, pos1, pos2, pos3, pos4, out):
+    nc = tc.nc
+    with ExitStack() as ctx:
+        lists = ctx.enter_context(tc.tile_pool(name="lists", bufs=1))
+        keep = ctx.enter_context(tc.tile_pool(name="keep", bufs=1))
+        psum = ctx.enter_context(tc.psum_pool(name="psum", bufs=1))
+
+        score_rows = keep.tile([P, P], F32, name="score_rows")
+        nc.sync.dma_start(out=score_rows[:], in_=score.rearrange("d p (h c) -> (d p h) c", c=P)[0 : P * ROW_STEP : ROW_STEP, :])
+        picks = lists.tile([P, S // 16], U16, name="picks")
+        nc.sync.dma_start(picks[:], offs)
+        x_planes = xT.rearrange("(p j) t -> j p t", j=PACK)
+        planes = []
+        for j in range(PACK):
+            plane = keep.tile([P, T], F32, name="plane%d" % j)
+            nc.sync.dma_start(out=plane[:], in_=x_planes[j])
+            planes.append(plane)
+        w_codes = keep.tile([P, N], U32, name="w_codes", align_bytes=64)
+        nc.sync.dma_start(out=w_codes[:].bitcast(I32), in_=w1_words[0].rearrange("p n t -> p (n t)").bitcast(I32))
+        w_scales = keep.tile([P, N], U8, name="w_scales", align_bytes=64)
+        nc.vector.memset(w_scales[:].bitcast(I32), 0)
+        for q in range(4):
+            nc.sync.dma_start(out=w_scales[32 * q : 32 * q + 4, :].bitcast(I32), in_=w1_scales[0, 4 * q : 4 * q + 4, :].bitcast(I32))
+        places = []
+        for d, pos in enumerate((pos1, pos2, pos3, pos4)):
+            place = lists.tile([P, V // 16], U16, name="place%d" % d)
+            nc.sync.dma_start(place[:], pos)
+            places.append(place)
+
+        warm_in = keep.tile([P, 1], F32, name="warm_in")
+        warm_out = keep.tile([P, 1], F32, name="warm_out")
+        nc.vector.memset(warm_in[:], 0.0)
+        nc.scalar.activation(warm_out[:], warm_in[:], ACT.Exp)
+
+        ident = keep.tile([P, P], F32, name="ident")
+        make_identity(nc, ident[:])
+
+        score_bank = psum.tile([P, 512], F32, name="score_bank")
+        nc.tensor.transpose(score_bank[:, 0:P], score_rows[:], ident[:])
+        scores = score_bank[:, 0 : D * D_STEP].rearrange("p (d r) -> p r d", r=D_STEP)[:, 0:2, :]
+        neg_max = keep.tile([P, 2], F32, name="neg_max")
+        nc.vector.tensor_reduce(neg_max[:], scores, mybir.AxisListType.X, ALU.max, negate=True)
+        exps = keep.tile([P, 2, D], F32, name="exps")
+        sums = keep.tile([P, 2], F32, name="sums")
+        for h in range(2):
+            nc.scalar.activation(exps[:, h, :], scores[:, h, :], ACT.Exp, bias=neg_max[:, h : h + 1], accum_out=sums[:, h : h + 1])
+        inv_sums = keep.tile([P, 2], F32, name="inv_sums")
+        nc.vector.reciprocal(inv_sums[:], sums[:])
+        shares = keep.tile([P, 2, D], F32, name="shares")
+        for h in range(2):
+            nc.scalar.activation(shares[:, h, :], exps[:, h, :], ACT.Copy, scale=inv_sums[:, h : h + 1])
+        weights = keep.tile([P, D, V], F32, name="weights")
+        for pair in range(2):
+            spread = psum.tile([P, 2, V], F32, name="spread%d" % pair)
+            for e in range(2):
+                for h in range(2):
+                    d = 2 * pair + e
+                    nc.tensor.transpose(spread[:, e, h * P : (h + 1) * P], shares[:, h, d : d + 1].to_broadcast([P, P]), ident[:])
+            nc.scalar.copy(weights[:, 2 * pair : 2 * pair + 2, :], spread[:])
+
+        low = keep.tile([P, 2, S], F32, name="low")
+        high = keep.tile([P, 2, S], F32, name="high")
+        grouped = keep.tile([P, S, PACK], BF16, name="grouped", align_bytes=64)
+        halves = [slice(0, HALF), slice(HALF, S)]
+        cols = [slice(0, HALF // 16), slice(HALF // 16, S // 16)]
+
+        nc.vector.tensor_copy(low[:, 0, :], planes[0][:].indirect(picks[:]))
+        for h in range(2):
+            nc.vector.tensor_copy(low[:, 1, halves[h]], planes[1][:].indirect(picks[:, cols[h]]))
+            nc.scalar.copy(grouped[:, halves[h], 0:2], low[:, :, halves[h]].rearrange("p j c -> p c j"))
+        nc.vector.tensor_copy(high[:, 0, :], planes[2][:].indirect(picks[:]))
+        for h in range(2):
+            nc.vector.tensor_copy(high[:, 1, halves[h]], planes[3][:].indirect(picks[:, cols[h]]))
+        nc.scalar.copy(grouped[:, halves[0], 2:4], high[:, :, halves[0]].rearrange("p j c -> p c j"))
+        nc.vector.tensor_copy(grouped[:, halves[1], 2:4], high[:, :, halves[1]].rearrange("p j c -> p c j"))
+
+        x_codes = keep.tile([P, S], U32, name="x_codes", align_bytes=64)
+        x_scales = keep.tile([P, S], U8, name="x_scales", align_bytes=64)
+        y = keep.tile([P, S], F32, name="y")
+        for h in range(2):
+            nc.vector.quantize_mx(
+                out=x_codes[:, halves[h]].bitcast(FP8X4),
+                scales=x_scales[:, halves[h]],
+                in_=grouped[:, halves[h], :].rearrange("p c j -> p (c j)"),
+            )
+        for h in range(2):
+            acc = psum.tile([P, HALF], F32, name="acc%d" % h)
+            nc.tensor.matmul_mx(
+                out=acc[:],
+                lhsT=w_codes[:].bitcast(FP8X4),
+                lhsT_scale=w_scales[:],
+                rhs=x_codes[:, halves[h]].bitcast(FP8X4),
+                rhs_scale=x_scales[:, halves[h]],
+                start=True,
+                stop=True,
+            )
+            if h == 0:
+                nc.scalar.copy(y[:, halves[h]], acc[:])
+            else:
+                nc.vector.tensor_copy(y[:, halves[h]], acc[:])
+
+        terms = keep.tile([P, D, V], F32, name="terms")
+        sum01 = keep.tile([P, V], F32, name="sum01")
+        sum012 = keep.tile([P, V], F32, name="sum012")
+        result = keep.tile([P, V], F32, name="result")
+        for d in range(3):
+            nc.vector.tensor_tensor(terms[:, d, :], y[:].indirect(places[d][:]), weights[:, d, :], ALU.mult)
+        nc.vector.tensor_tensor(sum01[:], terms[:, 0, :], terms[:, 1, :], ALU.add)
+        nc.vector.tensor_tensor(terms[:, 3, :], y[:].indirect(places[3][:]), weights[:, 3, :], ALU.mult)
+        for h in range(2):
+            c = slice(h * P, (h + 1) * P)
+            nc.vector.tensor_tensor(sum012[:, c], sum01[:, c], terms[:, 2, c], ALU.add)
+        for h in range(2):
+            c = slice(h * P, (h + 1) * P)
+            nc.vector.tensor_tensor(result[:, c], sum012[:, c], terms[:, 3, c], ALU.add)
+            (nc.scalar if h == 0 else nc.sync).dma_start(out=out[:, c], in_=result[:, c])

@@ -17,8 +17,10 @@ P = 128
 K, T, S, D, V, N = 512, 1024, 512, 4, 256, 128
 PACK = 4
 HALF = S // 2
-ROW_STEP = 7
-D_STEP = 38
+PIECES = ((0, 256), (256, 384), (384, 512))
+SCALAR_SHARE = 160
+ROW_STEP = 33
+D_STEP = 8
 
 FLOPS = 2 * K * S * N
 BYTES = 4 * K * T + K * N + K * N // 32 + 4 * D * V + 2 * (S + D * V) + 4 * N * V
@@ -32,19 +34,20 @@ def tile_picked_gatv_none_e_kernel(tc, xT, w1_words, w1_scales, score, offs, pos
         psum = ctx.enter_context(tc.psum_pool(name="psum", bufs=1))
 
         score_rows = keep.tile([P, P], F32, name="score_rows")
-        nc.sync.dma_start(out=score_rows[:], in_=score.rearrange("d p (h c) -> (d p h) c", c=P)[0 : P * ROW_STEP : ROW_STEP, :])
+        nc.sync.dma_start(out=score_rows[0:32, :], in_=score.rearrange("d p (h c) -> (d p h) c", c=P)[0 : D * P * 2 : ROW_STEP, :])
+        nc.gpsimd.memset(score_rows[32:64, :], 0.0)
+        nc.gpsimd.memset(score_rows[64:128, :], 0.0)
+        x_planes = xT.rearrange("(p j) t -> j p t", j=PACK)
+        planes = [keep.tile([P, T], F32, name="plane%d" % j) for j in range(PACK)]
+        nc.sync.dma_start(out=planes[0][:], in_=x_planes[0])
         picks = lists.tile([P, S // 16], U16, name="picks")
         nc.sync.dma_start(picks[:], offs)
-        x_planes = xT.rearrange("(p j) t -> j p t", j=PACK)
-        planes = []
-        for j in range(PACK):
-            plane = keep.tile([P, T], F32, name="plane%d" % j)
-            nc.sync.dma_start(out=plane[:], in_=x_planes[j])
-            planes.append(plane)
+        for j in range(1, PACK):
+            nc.sync.dma_start(out=planes[j][:], in_=x_planes[j])
         w_codes = keep.tile([P, N], U32, name="w_codes", align_bytes=64)
         nc.sync.dma_start(out=w_codes[:].bitcast(I32), in_=w1_words[0].rearrange("p n t -> p (n t)").bitcast(I32))
         w_scales = keep.tile([P, N], U8, name="w_scales", align_bytes=64)
-        nc.vector.memset(w_scales[:].bitcast(I32), 0)
+        nc.gpsimd.memset(w_scales[:].bitcast(I32), 0)
         for q in range(4):
             nc.sync.dma_start(out=w_scales[32 * q : 32 * q + 4, :].bitcast(I32), in_=w1_scales[0, 4 * q : 4 * q + 4, :].bitcast(I32))
         places = []
@@ -53,86 +56,95 @@ def tile_picked_gatv_none_e_kernel(tc, xT, w1_words, w1_scales, score, offs, pos
             nc.sync.dma_start(place[:], pos)
             places.append(place)
 
-        warm_in = keep.tile([P, 1], F32, name="warm_in")
-        warm_out = keep.tile([P, 1], F32, name="warm_out")
-        nc.vector.memset(warm_in[:], 0.0)
-        nc.scalar.activation(warm_out[:], warm_in[:], ACT.Exp)
-
         ident = keep.tile([P, P], F32, name="ident")
         make_identity(nc, ident[:])
 
-        score_bank = psum.tile([P, 512], F32, name="score_bank")
-        nc.tensor.transpose(score_bank[:, 0:P], score_rows[:], ident[:])
+        picked = keep.tile([P, PACK, S], F32, name="picked")
+
+        def gather(j, a, b):
+            nc.vector.tensor_copy(picked[:, j, a:b], planes[j][:].indirect(picks[:, a // 16 : b // 16]))
+
+        def pair_up(engine_copy, j, a, b):
+            engine_copy(grouped[:, a:b, j : j + 2], picked[:, j : j + 2, a:b].rearrange("p j c -> p c j"))
+
+        largest = picked[:, 0, S - 2 : S]
+        sums = picked[:, 1, 0:S:HALF]
+        exps = picked[:, 2:4, 0 : S : S // D]
+
+        score_bank = psum.tile([P, P], F32, name="score_bank")
+        nc.tensor.transpose(score_bank[:], score_rows[:], ident[:])
         scores = score_bank[:, 0 : D * D_STEP].rearrange("p (d r) -> p r d", r=D_STEP)[:, 0:2, :]
-        neg_max = keep.tile([P, 2], F32, name="neg_max")
-        nc.vector.tensor_reduce(neg_max[:], scores, mybir.AxisListType.X, ALU.max, negate=True)
-        exps = keep.tile([P, 2, D], F32, name="exps")
-        sums = keep.tile([P, 2], F32, name="sums")
+        nc.vector.tensor_reduce(largest, scores, mybir.AxisListType.X, ALU.max)
+        shifted = keep.tile([P, 2, D], F32, name="shifted", tag="slot_a")
+        nc.vector.tensor_tensor(shifted[:], scores, largest.unsqueeze(2).to_broadcast([P, 2, D]), ALU.subtract)
         for h in range(2):
-            nc.scalar.activation(exps[:, h, :], scores[:, h, :], ACT.Exp, bias=neg_max[:, h : h + 1], accum_out=sums[:, h : h + 1])
-        inv_sums = keep.tile([P, 2], F32, name="inv_sums")
-        nc.vector.reciprocal(inv_sums[:], sums[:])
+            nc.scalar.activation(exps[:, h, :], shifted[:, h, :], ACT.Exp, accum_out=sums[:, h : h + 1])
+        gather(0, SCALAR_SHARE, S)
+        rounded = keep.tile([P, T], BF16, name="rounded", tag="slot_a")
+        nc.scalar.copy(rounded[:], planes[0][:])
+        inv_sums = keep.tile([P, 2], F32, name="inv_sums", tag="slot_b", align_bytes=64)
+        nc.vector.reciprocal(inv_sums[:], sums)
         shares = keep.tile([P, 2, D], F32, name="shares")
         for h in range(2):
             nc.scalar.activation(shares[:, h, :], exps[:, h, :], ACT.Copy, scale=inv_sums[:, h : h + 1])
-        weights = keep.tile([P, D, V], F32, name="weights")
+        grouped = keep.tile([P, S, PACK], BF16, name="grouped", tag="slot_b", align_bytes=64)
+        nc.scalar.activation(grouped[:, 0:SCALAR_SHARE, 0], rounded[:].indirect(picks[:, 0 : SCALAR_SHARE // 16]), ACT.Copy)
+        gather(1, 0, SCALAR_SHARE)
+        gather(1, SCALAR_SHARE, S)
+        nc.scalar.copy(grouped[:, 0:SCALAR_SHARE, 1], picked[:, 1, 0:SCALAR_SHARE])
+        pair_up(nc.scalar.copy, 0, SCALAR_SHARE, S)
+        spreads = []
         for pair in range(2):
             spread = psum.tile([P, 2, V], F32, name="spread%d" % pair)
             for e in range(2):
                 for h in range(2):
                     d = 2 * pair + e
                     nc.tensor.transpose(spread[:, e, h * P : (h + 1) * P], shares[:, h, d : d + 1].to_broadcast([P, P]), ident[:])
-            nc.scalar.copy(weights[:, 2 * pair : 2 * pair + 2, :], spread[:])
+            spreads.append(spread)
 
-        low = keep.tile([P, 2, S], F32, name="low")
-        high = keep.tile([P, 2, S], F32, name="high")
-        grouped = keep.tile([P, S, PACK], BF16, name="grouped", align_bytes=64)
-        halves = [slice(0, HALF), slice(HALF, S)]
-        cols = [slice(0, HALF // 16), slice(HALF // 16, S // 16)]
-
-        nc.vector.tensor_copy(low[:, 0, :], planes[0][:].indirect(picks[:]))
-        for h in range(2):
-            nc.vector.tensor_copy(low[:, 1, halves[h]], planes[1][:].indirect(picks[:, cols[h]]))
-            nc.scalar.copy(grouped[:, halves[h], 0:2], low[:, :, halves[h]].rearrange("p j c -> p c j"))
-        nc.vector.tensor_copy(high[:, 0, :], planes[2][:].indirect(picks[:]))
-        for h in range(2):
-            nc.vector.tensor_copy(high[:, 1, halves[h]], planes[3][:].indirect(picks[:, cols[h]]))
-        nc.scalar.copy(grouped[:, halves[0], 2:4], high[:, :, halves[0]].rearrange("p j c -> p c j"))
-        nc.vector.tensor_copy(grouped[:, halves[1], 2:4], high[:, :, halves[1]].rearrange("p j c -> p c j"))
+        gather(2, 0, S)
+        for a, b in PIECES:
+            gather(3, a, b)
+        pair_up(nc.scalar.copy, 2, *PIECES[0])
+        for a, b in PIECES[1:]:
+            pair_up(nc.vector.tensor_copy, 2, a, b)
+        for pair in range(2):
+            nc.scalar.copy(picked[:, 2:4, pair * V : (pair + 1) * V], spreads[pair][:])
+        weights = [picked[:, 2 + d % 2, (d // 2) * V : (d // 2 + 1) * V] for d in range(D)]
 
         x_codes = keep.tile([P, S], U32, name="x_codes", align_bytes=64)
         x_scales = keep.tile([P, S], U8, name="x_scales", align_bytes=64)
         y = keep.tile([P, S], F32, name="y")
-        for h in range(2):
+        for a, b in PIECES:
             nc.vector.quantize_mx(
-                out=x_codes[:, halves[h]].bitcast(FP8X4),
-                scales=x_scales[:, halves[h]],
-                in_=grouped[:, halves[h], :].rearrange("p c j -> p (c j)"),
+                out=x_codes[:, a:b].bitcast(FP8X4),
+                scales=x_scales[:, a:b],
+                in_=grouped[:, a:b, :].rearrange("p c j -> p (c j)"),
             )
-        for h in range(2):
-            acc = psum.tile([P, HALF], F32, name="acc%d" % h)
+        for i, (a, b) in enumerate(PIECES):
+            acc = psum.tile([P, b - a], F32, name="acc%d" % i)
             nc.tensor.matmul_mx(
                 out=acc[:],
                 lhsT=w_codes[:].bitcast(FP8X4),
                 lhsT_scale=w_scales[:],
-                rhs=x_codes[:, halves[h]].bitcast(FP8X4),
-                rhs_scale=x_scales[:, halves[h]],
+                rhs=x_codes[:, a:b].bitcast(FP8X4),
+                rhs_scale=x_scales[:, a:b],
                 start=True,
                 stop=True,
             )
-            if h == 0:
-                nc.scalar.copy(y[:, halves[h]], acc[:])
+            if b < S:
+                nc.scalar.copy(y[:, a:b], acc[:])
             else:
-                nc.vector.tensor_copy(y[:, halves[h]], acc[:])
+                nc.vector.tensor_copy(y[:, a:b], acc[:])
 
         terms = keep.tile([P, D, V], F32, name="terms")
         sum01 = keep.tile([P, V], F32, name="sum01")
         sum012 = keep.tile([P, V], F32, name="sum012")
         result = keep.tile([P, V], F32, name="result")
         for d in range(3):
-            nc.vector.tensor_tensor(terms[:, d, :], y[:].indirect(places[d][:]), weights[:, d, :], ALU.mult)
+            nc.vector.tensor_tensor(terms[:, d, :], y[:].indirect(places[d][:]), weights[d], ALU.mult)
         nc.vector.tensor_tensor(sum01[:], terms[:, 0, :], terms[:, 1, :], ALU.add)
-        nc.vector.tensor_tensor(terms[:, 3, :], y[:].indirect(places[3][:]), weights[:, 3, :], ALU.mult)
+        nc.vector.tensor_tensor(terms[:, 3, :], y[:].indirect(places[3][:]), weights[3], ALU.mult)
         for h in range(2):
             c = slice(h * P, (h + 1) * P)
             nc.vector.tensor_tensor(sum012[:, c], sum01[:, c], terms[:, 2, c], ALU.add)

@@ -105,22 +105,21 @@ def tile_picked_gatv_none_e_kernel(tc, xT, w1_words, w1_scales, score, offs, pos
         gather(2, 0, S)
         for a, b in PIECES:
             gather(3, a, b)
-        pair_up(nc.scalar.copy, 2, *PIECES[0])
-        for a, b in PIECES[1:]:
-            pair_up(nc.vector.tensor_copy, 2, a, b)
+        for engine_copy, (a, b) in zip((nc.scalar.copy, nc.vector.tensor_copy, nc.vector.tensor_copy), PIECES):
+            pair_up(engine_copy, 2, a, b)
         for pair in range(2):
-            nc.scalar.copy(picked[:, 2:4, pair * V : (pair + 1) * V], spreads[pair][:])
-        weights = [picked[:, 2 + d % 2, (d // 2) * V : (d // 2 + 1) * V] for d in range(D)]
+            nc.scalar.copy(picked[:, 2 + pair, :], spreads[pair][:].rearrange("p e v -> p (e v)"))
+        weights = [picked[:, 2 + d // 2, (d % 2) * V : (d % 2 + 1) * V] for d in range(D)]
 
         x_codes = keep.tile([P, S], U32, name="x_codes", align_bytes=64)
         x_scales = keep.tile([P, S], U8, name="x_scales", align_bytes=64)
-        y = keep.tile([P, S], F32, name="y")
         for a, b in PIECES:
             nc.vector.quantize_mx(
                 out=x_codes[:, a:b].bitcast(FP8X4),
                 scales=x_scales[:, a:b],
                 in_=grouped[:, a:b, :].rearrange("p c j -> p (c j)"),
             )
+        y = keep.tile([P, S], F32, name="y", tag="slot_b", align_bytes=64)
         for i, (a, b) in enumerate(PIECES):
             acc = psum.tile([P, b - a], F32, name="acc%d" % i)
             nc.tensor.matmul_mx(
@@ -132,10 +131,7 @@ def tile_picked_gatv_none_e_kernel(tc, xT, w1_words, w1_scales, score, offs, pos
                 start=True,
                 stop=True,
             )
-            if b < S:
-                nc.scalar.copy(y[:, a:b], acc[:])
-            else:
-                nc.vector.tensor_copy(y[:, a:b], acc[:])
+            nc.vector.tensor_copy(y[:, a:b], acc[:])
 
         terms = keep.tile([P, D, V], F32, name="terms")
         sum01 = keep.tile([P, V], F32, name="sum01")

@@ -17,10 +17,9 @@ P = 128
 K, T, S, D, V, N = 512, 1024, 512, 4, 256, 128
 PACK = 4
 HALF = S // 2
-PIECES = ((0, 256), (256, 384), (384, 512))
-SCALAR_SHARE = 160
-ROW_STEP = 33
-D_STEP = 8
+SCALAR_SHARE = 128
+ROW_STEP = 129
+ROW0 = 120
 
 FLOPS = 2 * K * S * N
 BYTES = 4 * K * T + K * N + K * N // 32 + 4 * D * V + 2 * (S + D * V) + 4 * N * V
@@ -34,9 +33,8 @@ def tile_picked_gatv_none_e_kernel(tc, xT, w1_words, w1_scales, score, offs, pos
         psum = ctx.enter_context(tc.psum_pool(name="psum", bufs=1))
 
         score_rows = keep.tile([P, P], F32, name="score_rows")
-        nc.sync.dma_start(out=score_rows[0:32, :], in_=score.rearrange("d p (h c) -> (d p h) c", c=P)[0 : D * P * 2 : ROW_STEP, :])
-        nc.gpsimd.memset(score_rows[32:64, :], 0.0)
-        nc.gpsimd.memset(score_rows[64:128, :], 0.0)
+        nc.sync.dma_start(out=score_rows[ROW0:P, :], in_=score.rearrange("d p (h c) -> (d p h) c", c=P)[0 : D * P * 2 : ROW_STEP, :])
+        nc.gpsimd.memset(score_rows[0:ROW0, :], 0.0)
         x_planes = xT.rearrange("(p j) t -> j p t", j=PACK)
         planes = [keep.tile([P, T], F32, name="plane%d" % j) for j in range(PACK)]
         nc.sync.dma_start(out=planes[0][:], in_=x_planes[0])
@@ -59,7 +57,26 @@ def tile_picked_gatv_none_e_kernel(tc, xT, w1_words, w1_scales, score, offs, pos
         ident = keep.tile([P, P], F32, name="ident")
         make_identity(nc, ident[:])
 
-        picked = keep.tile([P, PACK, S], F32, name="picked")
+        score_bank = psum.tile([P, P], F32, name="score_bank", tag="bank_a")
+        nc.tensor.transpose(score_bank[:], score_rows[:], ident[:])
+        scores = score_bank[:, ROW0:P].rearrange("p (d r) -> p r d", r=2)
+        minus_largest = keep.tile([P, 2], F32, name="minus_largest")
+        nc.vector.tensor_reduce(minus_largest[:], scores, mybir.AxisListType.X, ALU.max, negate=True)
+        exps = keep.tile([P, 2, D], F32, name="exps", tag="slot_a")
+        sums = keep.tile([P, 2], F32, name="sums", tag="slot_b")
+        for h in range(2):
+            nc.scalar.activation(exps[:, h, :], scores[:, h, :], ACT.Exp, bias=minus_largest[:, h : h + 1], accum_out=sums[:, h : h + 1])
+        inv_sums = keep.tile([P, 2], F32, name="inv_sums")
+        nc.vector.reciprocal(inv_sums[:], sums[:])
+        shares = keep.tile([P, 2, D], F32, name="shares")
+        for h in range(2):
+            nc.scalar.activation(shares[:, h, :], exps[:, h, :], ACT.Copy, scale=inv_sums[:, h : h + 1])
+        spread = psum.tile([P, D, P], F32, name="spread", tag="bank_b")
+        for d in range(D):
+            nc.tensor.transpose(spread[:, d, :], shares[:, 1, d : d + 1].to_broadcast([P, P]), ident[:])
+
+        picked = keep.tile([P, PACK, S], F32, name="picked", tag="slot_b")
+        grouped = keep.tile([P, S, PACK], BF16, name="grouped", align_bytes=64)
 
         def gather(j, a, b):
             nc.vector.tensor_copy(picked[:, j, a:b], planes[j][:].indirect(picks[:, a // 16 : b // 16]))
@@ -67,61 +84,27 @@ def tile_picked_gatv_none_e_kernel(tc, xT, w1_words, w1_scales, score, offs, pos
         def pair_up(engine_copy, j, a, b):
             engine_copy(grouped[:, a:b, j : j + 2], picked[:, j : j + 2, a:b].rearrange("p j c -> p c j"))
 
-        largest = picked[:, 0, S - 2 : S]
-        sums = picked[:, 1, 0:S:HALF]
-        exps = picked[:, 2:4, 0 : S : S // D]
-
-        score_bank = psum.tile([P, P], F32, name="score_bank")
-        nc.tensor.transpose(score_bank[:], score_rows[:], ident[:])
-        scores = score_bank[:, 0 : D * D_STEP].rearrange("p (d r) -> p r d", r=D_STEP)[:, 0:2, :]
-        nc.vector.tensor_reduce(largest, scores, mybir.AxisListType.X, ALU.max)
-        shifted = keep.tile([P, 2, D], F32, name="shifted", tag="slot_a")
-        nc.vector.tensor_tensor(shifted[:], scores, largest.unsqueeze(2).to_broadcast([P, 2, D]), ALU.subtract)
-        for h in range(2):
-            nc.scalar.activation(exps[:, h, :], shifted[:, h, :], ACT.Exp, accum_out=sums[:, h : h + 1])
-        gather(0, SCALAR_SHARE, S)
-        rounded = keep.tile([P, T], BF16, name="rounded", tag="slot_a")
-        nc.scalar.copy(rounded[:], planes[0][:])
-        inv_sums = keep.tile([P, 2], F32, name="inv_sums", tag="slot_b", align_bytes=64)
-        nc.vector.reciprocal(inv_sums[:], sums)
-        shares = keep.tile([P, 2, D], F32, name="shares")
-        for h in range(2):
-            nc.scalar.activation(shares[:, h, :], exps[:, h, :], ACT.Copy, scale=inv_sums[:, h : h + 1])
-        grouped = keep.tile([P, S, PACK], BF16, name="grouped", tag="slot_b", align_bytes=64)
-        nc.scalar.activation(grouped[:, 0:SCALAR_SHARE, 0], rounded[:].indirect(picks[:, 0 : SCALAR_SHARE // 16]), ACT.Copy)
-        gather(1, 0, SCALAR_SHARE)
+        gather(0, 0, S)
         gather(1, SCALAR_SHARE, S)
-        nc.scalar.copy(grouped[:, 0:SCALAR_SHARE, 1], picked[:, 1, 0:SCALAR_SHARE])
+        nc.scalar.copy(grouped[:, 0:SCALAR_SHARE, 0], picked[:, 0, 0:SCALAR_SHARE])
+        rounded = keep.tile([P, T], BF16, name="rounded", tag="slot_a")
+        nc.scalar.copy(rounded[:], planes[1][:])
+        nc.scalar.activation(grouped[:, 0:SCALAR_SHARE, 1], rounded[:].indirect(picks[:, 0 : SCALAR_SHARE // 16]), ACT.Copy)
         pair_up(nc.scalar.copy, 0, SCALAR_SHARE, S)
-        spreads = []
-        for pair in range(2):
-            spread = psum.tile([P, 2, V], F32, name="spread%d" % pair)
-            for e in range(2):
-                for h in range(2):
-                    d = 2 * pair + e
-                    nc.tensor.transpose(spread[:, e, h * P : (h + 1) * P], shares[:, h, d : d + 1].to_broadcast([P, P]), ident[:])
-            spreads.append(spread)
 
-        gather(2, 0, S)
-        for a, b in PIECES:
-            gather(3, a, b)
-        for engine_copy, (a, b) in zip((nc.scalar.copy, nc.vector.tensor_copy, nc.vector.tensor_copy), PIECES):
-            pair_up(engine_copy, 2, a, b)
-        for pair in range(2):
-            nc.scalar.copy(picked[:, 2 + pair, :], spreads[pair][:].rearrange("p e v -> p (e v)"))
-        weights = [picked[:, 2 + d // 2, (d % 2) * V : (d % 2 + 1) * V] for d in range(D)]
-
-        x_codes = keep.tile([P, S], U32, name="x_codes", align_bytes=64)
+        x_codes = keep.tile([P, S], U32, name="x_codes", tag="slot_c", align_bytes=64)
         x_scales = keep.tile([P, S], U8, name="x_scales", align_bytes=64)
-        for a, b in PIECES:
+        y = keep.tile([P, S], F32, name="y")
+
+        def quantise(a, b):
             nc.vector.quantize_mx(
                 out=x_codes[:, a:b].bitcast(FP8X4),
                 scales=x_scales[:, a:b],
                 in_=grouped[:, a:b, :].rearrange("p c j -> p (c j)"),
             )
-        y = keep.tile([P, S], F32, name="y", tag="slot_b", align_bytes=64)
-        for i, (a, b) in enumerate(PIECES):
-            acc = psum.tile([P, b - a], F32, name="acc%d" % i)
+
+        def project(engine_copy, a, b):
+            acc = psum.tile([P, b - a], F32, name="acc%d" % a)
             nc.tensor.matmul_mx(
                 out=acc[:],
                 lhsT=w_codes[:].bitcast(FP8X4),
@@ -131,20 +114,54 @@ def tile_picked_gatv_none_e_kernel(tc, xT, w1_words, w1_scales, score, offs, pos
                 start=True,
                 stop=True,
             )
-            nc.vector.tensor_copy(y[:, a:b], acc[:])
+            engine_copy(y[:, a:b], acc[:])
 
-        terms = keep.tile([P, D, V], F32, name="terms")
-        sum01 = keep.tile([P, V], F32, name="sum01")
-        sum012 = keep.tile([P, V], F32, name="sum012")
+        gather(2, 0, S)
+        gather(3, 0, 128)
+        pair_up(nc.scalar.copy, 2, 0, 128)
+        gather(3, 256, 384)
+        gather(3, 128, 256)
+        pair_up(nc.scalar.copy, 2, 128, 256)
+        pair_up(nc.vector.tensor_copy, 2, 256, 384)
+        gather(3, 384, 512)
+        pair_up(nc.scalar.copy, 2, 384, 512)
+        quantise(256, 384)
+        quantise(0, 256)
+        quantise(384, 512)
+        project(nc.scalar.copy, 256, 384)
+        project(nc.scalar.copy, 0, 256)
+        project(nc.vector.tensor_copy, 384, 512)
+
+        weights = keep.tile([P, D, P], F32, name="weights", tag="slot_c", align_bytes=64)
+        nc.scalar.copy(weights[:], spread[:])
+        fetched = keep.tile([P, D, P], F32, name="fetched")
+        turned = keep.tile([P, D, P], F32, name="turned")
+        terms = keep.tile([P, D, P], F32, name="terms")
+        sum01 = keep.tile([P, P], F32, name="sum01")
+        sum012 = keep.tile([P, P], F32, name="sum012")
         result = keep.tile([P, V], F32, name="result")
+        cols = P // 16
+
+        back = psum.tile([P, P], F32, name="back")
+        for d in range(D):
+            nc.vector.tensor_copy(fetched[:, d, :], y[:].indirect(places[d][:, 0:cols]))
+            forth = psum.tile([P, P], F32, name="forth%d" % d, tag=("bank_a", "bank_c", "bank_d", "bank_b")[d])
+            nc.tensor.transpose(forth[:], fetched[:, d, :], ident[:])
+            nc.scalar.activation(turned[:, d, :], forth[:], ACT.Copy, scale=shares[:, 0, d : d + 1])
+        for d in range(D):
+            nc.tensor.matmul(back[:], lhsT=turned[:, d, :], rhs=ident[:], start=(d == 0), stop=(d == D - 1), is_transpose=True)
+        nc.scalar.copy(result[:, 0:P], back[:])
+        nc.scalar.dma_start(out=out[:, 0:P], in_=result[:, 0:P])
+
+        def weigh(d):
+            nc.vector.tensor_tensor(terms[:, d, :], y[:].indirect(places[d][:, cols : 2 * cols]), weights[:, d, :], ALU.mult)
+
         for d in range(3):
-            nc.vector.tensor_tensor(terms[:, d, :], y[:].indirect(places[d][:]), weights[d], ALU.mult)
+            weigh(d)
         nc.vector.tensor_tensor(sum01[:], terms[:, 0, :], terms[:, 1, :], ALU.add)
-        nc.vector.tensor_tensor(terms[:, 3, :], y[:].indirect(places[3][:]), weights[3], ALU.mult)
-        for h in range(2):
-            c = slice(h * P, (h + 1) * P)
-            nc.vector.tensor_tensor(sum012[:, c], sum01[:, c], terms[:, 2, c], ALU.add)
-        for h in range(2):
-            c = slice(h * P, (h + 1) * P)
-            nc.vector.tensor_tensor(result[:, c], sum012[:, c], terms[:, 3, c], ALU.add)
-            (nc.scalar if h == 0 else nc.sync).dma_start(out=out[:, c], in_=result[:, c])
+        weigh(3)
+        for c in (0, P // 2):
+            nc.vector.tensor_tensor(sum012[:, c : c + P // 2], sum01[:, c : c + P // 2], terms[:, 2, c : c + P // 2], ALU.add)
+        for c in (0, P // 2):
+            nc.vector.tensor_tensor(result[:, P + c : P + c + P // 2], sum012[:, c : c + P // 2], terms[:, 3, c : c + P // 2], ALU.add)
+        nc.sync.dma_start(out=out[:, P:V], in_=result[:, P:V])

@@ -17,7 +17,7 @@ P = 128
 K, T, S, D, V, N = 512, 1024, 512, 4, 256, 128
 PACK = 4
 HALF = S // 2
-SCALAR_SHARE = 128
+SCALAR_SHARE = 160
 ROW_STEP = 129
 ROW0 = 120
 
@@ -33,19 +33,18 @@ def tile_picked_gatv_none_e_kernel(tc, xT, w1_words, w1_scales, score, offs, pos
         psum = ctx.enter_context(tc.psum_pool(name="psum", bufs=1))
 
         score_rows = keep.tile([P, P], F32, name="score_rows")
-        nc.sync.dma_start(out=score_rows[ROW0:P, :], in_=score.rearrange("d p (h c) -> (d p h) c", c=P)[0 : D * P * 2 : ROW_STEP, :])
-        nc.gpsimd.memset(score_rows[0:ROW0, :], 0.0)
+        nc.scalar.dma_start(out=score_rows[ROW0:P, :], in_=score.rearrange("d p (h c) -> (d p h) c", c=P)[0 : D * P * 2 : ROW_STEP, :])
+        nc.vector.memset(score_rows[0:ROW0, :], 0.0)
         x_planes = xT.rearrange("(p j) t -> j p t", j=PACK)
         planes = [keep.tile([P, T], F32, name="plane%d" % j) for j in range(PACK)]
-        nc.sync.dma_start(out=planes[0][:], in_=x_planes[0])
         picks = lists.tile([P, S // 16], U16, name="picks")
         nc.sync.dma_start(picks[:], offs)
-        for j in range(1, PACK):
+        for j in range(PACK):
             nc.sync.dma_start(out=planes[j][:], in_=x_planes[j])
         w_codes = keep.tile([P, N], U32, name="w_codes", align_bytes=64)
         nc.sync.dma_start(out=w_codes[:].bitcast(I32), in_=w1_words[0].rearrange("p n t -> p (n t)").bitcast(I32))
         w_scales = keep.tile([P, N], U8, name="w_scales", align_bytes=64)
-        nc.gpsimd.memset(w_scales[:].bitcast(I32), 0)
+        nc.vector.memset(w_scales[:].bitcast(I32), 0)
         for q in range(4):
             nc.sync.dma_start(out=w_scales[32 * q : 32 * q + 4, :].bitcast(I32), in_=w1_scales[0, 4 * q : 4 * q + 4, :].bitcast(I32))
         places = []
@@ -84,13 +83,15 @@ def tile_picked_gatv_none_e_kernel(tc, xT, w1_words, w1_scales, score, offs, pos
         def pair_up(engine_copy, j, a, b):
             engine_copy(grouped[:, a:b, j : j + 2], picked[:, j : j + 2, a:b].rearrange("p j c -> p c j"))
 
-        gather(0, 0, S)
-        gather(1, SCALAR_SHARE, S)
-        nc.scalar.copy(grouped[:, 0:SCALAR_SHARE, 0], picked[:, 0, 0:SCALAR_SHARE])
+        gather(0, SCALAR_SHARE, S)
         rounded = keep.tile([P, T], BF16, name="rounded", tag="slot_a")
-        nc.scalar.copy(rounded[:], planes[1][:])
-        nc.scalar.activation(grouped[:, 0:SCALAR_SHARE, 1], rounded[:].indirect(picks[:, 0 : SCALAR_SHARE // 16]), ACT.Copy)
-        pair_up(nc.scalar.copy, 0, SCALAR_SHARE, S)
+        nc.scalar.copy(rounded[:], planes[0][:])
+        nc.scalar.activation(grouped[:, 0:SCALAR_SHARE, 0], rounded[:].indirect(picks[:, 0 : SCALAR_SHARE // 16]), ACT.Copy)
+        gather(1, 0, HALF)
+        nc.scalar.copy(grouped[:, 0:SCALAR_SHARE, 1], picked[:, 1, 0:SCALAR_SHARE])
+        pair_up(nc.scalar.copy, 0, SCALAR_SHARE, HALF)
+        gather(1, HALF, S)
+        pair_up(nc.scalar.copy, 0, HALF, S)
 
         x_codes = keep.tile([P, S], U32, name="x_codes", tag="slot_c", align_bytes=64)
         x_scales = keep.tile([P, S], U8, name="x_scales", align_bytes=64)

@@ -17,7 +17,9 @@ P = 128
 K, T, S, D, V, N = 512, 1024, 512, 4, 256, 128
 PACK = 4
 HALF = S // 2
-SCALAR_SHARE = 160
+DIRECT = 384
+GROUPED_BYTES = S * PACK * 2
+LATE_A_BYTES = 2 * HALF * 4
 ROW_STEP = 129
 ROW0 = 120
 
@@ -30,9 +32,11 @@ def tile_picked_gatv_none_e_kernel(tc, xT, w1_words, w1_scales, score, offs, pos
     with ExitStack() as ctx:
         lists = ctx.enter_context(tc.tile_pool(name="lists", bufs=1))
         keep = ctx.enter_context(tc.tile_pool(name="keep", bufs=1))
+        late = ctx.enter_context(tc.tile_pool(name="late", bufs=1))
         psum = ctx.enter_context(tc.psum_pool(name="psum", bufs=1))
 
-        score_rows = keep.tile([P, P], F32, name="score_rows")
+        early = keep.tile([P, 2, S], F32, name="early")
+        score_rows = early[:, 0, 0:P]
         nc.scalar.dma_start(out=score_rows[ROW0:P, :], in_=score.rearrange("d p (h c) -> (d p h) c", c=P)[0 : D * P * 2 : ROW_STEP, :])
         nc.vector.memset(score_rows[0:ROW0, :], 0.0)
         x_planes = xT.rearrange("(p j) t -> j p t", j=PACK)
@@ -57,16 +61,22 @@ def tile_picked_gatv_none_e_kernel(tc, xT, w1_words, w1_scales, score, offs, pos
         make_identity(nc, ident[:])
 
         score_bank = psum.tile([P, P], F32, name="score_bank", tag="bank_a")
-        nc.tensor.transpose(score_bank[:], score_rows[:], ident[:])
+        nc.tensor.transpose(score_bank[:], score_rows, ident[:])
         scores = score_bank[:, ROW0:P].rearrange("p (d r) -> p r d", r=2)
-        minus_largest = keep.tile([P, 2], F32, name="minus_largest")
-        nc.vector.tensor_reduce(minus_largest[:], scores, mybir.AxisListType.X, ALU.max, negate=True)
-        exps = keep.tile([P, 2, D], F32, name="exps", tag="slot_a")
-        sums = keep.tile([P, 2], F32, name="sums", tag="slot_b")
+        minus_largest = early[:, 1, 0:2]
+        sums = early[:, 1, HALF : HALF + 2]
+        nc.vector.tensor_reduce(minus_largest, scores, mybir.AxisListType.X, ALU.max, negate=True)
+        exps_room = late.tile([P, (LATE_A_BYTES + 128) // 4], F32, name="exps_room", offset=GROUPED_BYTES - 64, align_bytes=64)
+        exps = exps_room[:, 0 : 2 * D].rearrange("p (h d) -> p h d", h=2)
         for h in range(2):
             nc.scalar.activation(exps[:, h, :], scores[:, h, :], ACT.Exp, bias=minus_largest[:, h : h + 1], accum_out=sums[:, h : h + 1])
+
+        def gather(dst, j, a, b):
+            nc.vector.tensor_copy(dst, planes[j][:].indirect(picks[:, a // 16 : b // 16]))
+
+        gather(early[:, 0, :], 0, 0, S)
         inv_sums = keep.tile([P, 2], F32, name="inv_sums")
-        nc.vector.reciprocal(inv_sums[:], sums[:])
+        nc.vector.reciprocal(inv_sums[:], sums)
         shares = keep.tile([P, 2, D], F32, name="shares")
         for h in range(2):
             nc.scalar.activation(shares[:, h, :], exps[:, h, :], ACT.Copy, scale=inv_sums[:, h : h + 1])
@@ -74,64 +84,56 @@ def tile_picked_gatv_none_e_kernel(tc, xT, w1_words, w1_scales, score, offs, pos
         for d in range(D):
             nc.tensor.transpose(spread[:, d, :], shares[:, 1, d : d + 1].to_broadcast([P, P]), ident[:])
 
-        picked = keep.tile([P, PACK, S], F32, name="picked", tag="slot_b")
-        grouped = keep.tile([P, S, PACK], BF16, name="grouped", align_bytes=64)
+        grouped = late.tile([P, S, PACK], BF16, name="grouped", offset=0, align_bytes=64)
+        late_a = late.tile([P, 2, HALF], F32, name="late_a", offset=GROUPED_BYTES, align_bytes=64)
+        late_b = late.tile([P, 2, P], F32, name="late_b", offset=GROUPED_BYTES + LATE_A_BYTES, align_bytes=64)
 
-        def gather(j, a, b):
-            nc.vector.tensor_copy(picked[:, j, a:b], planes[j][:].indirect(picks[:, a // 16 : b // 16]))
+        def pair_up(j, a, b, src):
+            nc.scalar.copy(grouped[:, a:b, j : j + 2], src.rearrange("p j c -> p c j"))
 
-        def pair_up(engine_copy, j, a, b):
-            engine_copy(grouped[:, a:b, j : j + 2], picked[:, j : j + 2, a:b].rearrange("p j c -> p c j"))
+        for a in (0, HALF):
+            gather(early[:, 1, a : a + HALF], 1, a, a + HALF)
+            pair_up(0, a, a + HALF, early[:, :, a : a + HALF])
+        gather(late_a[:, 0, :], 2, 0, HALF)
+        gather(late_b[:, 0, :], 2, HALF, DIRECT)
+        gather(grouped[:, DIRECT:S, 2], 2, DIRECT, S)
+        for a in (0, P):
+            gather(late_a[:, 1, a : a + P], 3, a, a + P)
+            pair_up(2, a, a + P, late_a[:, :, a : a + P])
+        gather(late_b[:, 1, :], 3, HALF, DIRECT)
+        pair_up(2, HALF, DIRECT, late_b[:])
+        gather(grouped[:, DIRECT:S, 3], 3, DIRECT, S)
 
-        gather(0, SCALAR_SHARE, S)
-        rounded = keep.tile([P, T], BF16, name="rounded", tag="slot_a")
-        nc.scalar.copy(rounded[:], planes[0][:])
-        nc.scalar.activation(grouped[:, 0:SCALAR_SHARE, 0], rounded[:].indirect(picks[:, 0 : SCALAR_SHARE // 16]), ACT.Copy)
-        gather(1, 0, HALF)
-        nc.scalar.copy(grouped[:, 0:SCALAR_SHARE, 1], picked[:, 1, 0:SCALAR_SHARE])
-        pair_up(nc.scalar.copy, 0, SCALAR_SHARE, HALF)
-        gather(1, HALF, S)
-        pair_up(nc.scalar.copy, 0, HALF, S)
-
-        x_codes = keep.tile([P, S], U32, name="x_codes", tag="slot_c", align_bytes=64)
         x_scales = keep.tile([P, S], U8, name="x_scales", align_bytes=64)
         y = keep.tile([P, S], F32, name="y")
-
-        def quantise(a, b):
+        codes = {
+            0: keep.tile([P, P], U32, name="codes0", align_bytes=64),
+            P: keep.tile([P, P], U32, name="codes1", align_bytes=64),
+            HALF: keep.tile([P, P], U32, name="codes2", tag="slot_c", align_bytes=64),
+            DIRECT: late.tile([P, P], U32, name="codes3", offset=GROUPED_BYTES, align_bytes=64),
+        }
+        order = (0, P, DIRECT, HALF)
+        for a in order:
             nc.vector.quantize_mx(
-                out=x_codes[:, a:b].bitcast(FP8X4),
-                scales=x_scales[:, a:b],
-                in_=grouped[:, a:b, :].rearrange("p c j -> p (c j)"),
+                out=codes[a][:].bitcast(FP8X4),
+                scales=x_scales[:, a : a + P],
+                in_=grouped[:, a : a + P, :].rearrange("p c j -> p (c j)"),
             )
-
-        def project(engine_copy, a, b):
-            acc = psum.tile([P, b - a], F32, name="acc%d" % a)
+        for a in order:
+            acc = psum.tile([P, P], F32, name="acc%d" % a)
             nc.tensor.matmul_mx(
                 out=acc[:],
                 lhsT=w_codes[:].bitcast(FP8X4),
                 lhsT_scale=w_scales[:],
-                rhs=x_codes[:, a:b].bitcast(FP8X4),
-                rhs_scale=x_scales[:, a:b],
+                rhs=codes[a][:].bitcast(FP8X4),
+                rhs_scale=x_scales[:, a : a + P],
                 start=True,
                 stop=True,
             )
-            engine_copy(y[:, a:b], acc[:])
-
-        gather(2, 0, S)
-        gather(3, 0, 128)
-        pair_up(nc.scalar.copy, 2, 0, 128)
-        gather(3, 256, 384)
-        gather(3, 128, 256)
-        pair_up(nc.scalar.copy, 2, 128, 256)
-        pair_up(nc.vector.tensor_copy, 2, 256, 384)
-        gather(3, 384, 512)
-        pair_up(nc.scalar.copy, 2, 384, 512)
-        quantise(256, 384)
-        quantise(0, 256)
-        quantise(384, 512)
-        project(nc.scalar.copy, 256, 384)
-        project(nc.scalar.copy, 0, 256)
-        project(nc.vector.tensor_copy, 384, 512)
+            if a == order[-1]:
+                nc.vector.tensor_copy(y[:, a : a + P], acc[:])
+            else:
+                nc.scalar.copy(y[:, a : a + P], acc[:])
 
         weights = keep.tile([P, D, P], F32, name="weights", tag="slot_c", align_bytes=64)
         nc.scalar.copy(weights[:], spread[:])
@@ -146,7 +148,7 @@ def tile_picked_gatv_none_e_kernel(tc, xT, w1_words, w1_scales, score, offs, pos
         back = psum.tile([P, P], F32, name="back")
         for d in range(D):
             nc.vector.tensor_copy(fetched[:, d, :], y[:].indirect(places[d][:, 0:cols]))
-            forth = psum.tile([P, P], F32, name="forth%d" % d, tag=("bank_a", "bank_c", "bank_d", "bank_b")[d])
+            forth = psum.tile([P, P], F32, name="forth%d" % d, tag=("bank_a", "acc0", "acc128", "bank_b")[d])
             nc.tensor.transpose(forth[:], fetched[:, d, :], ident[:])
             nc.scalar.activation(turned[:, d, :], forth[:], ACT.Copy, scale=shares[:, 0, d : d + 1])
         for d in range(D):

@@ -17,9 +17,7 @@ P = 128
 K, T, S, D, V, N = 512, 1024, 512, 4, 256, 128
 PACK = 4
 HALF = S // 2
-DIRECT = 384
 GROUPED_BYTES = S * PACK * 2
-LATE_A_BYTES = 2 * HALF * 4
 ROW_STEP = 129
 ROW0 = 120
 
@@ -66,7 +64,7 @@ def tile_picked_gatv_none_e_kernel(tc, xT, w1_words, w1_scales, score, offs, pos
         minus_largest = early[:, 1, 0:2]
         sums = early[:, 1, HALF : HALF + 2]
         nc.vector.tensor_reduce(minus_largest, scores, mybir.AxisListType.X, ALU.max, negate=True)
-        exps_room = late.tile([P, (LATE_A_BYTES + 128) // 4], F32, name="exps_room", offset=GROUPED_BYTES - 64, align_bytes=64)
+        exps_room = late.tile([P, 128 // 4], F32, name="exps_room", offset=GROUPED_BYTES - 64, align_bytes=64)
         exps = exps_room[:, 0 : 2 * D].rearrange("p (h d) -> p h d", h=2)
         for h in range(2):
             nc.scalar.activation(exps[:, h, :], scores[:, h, :], ACT.Exp, bias=minus_largest[:, h : h + 1], accum_out=sums[:, h : h + 1])
@@ -86,7 +84,6 @@ def tile_picked_gatv_none_e_kernel(tc, xT, w1_words, w1_scales, score, offs, pos
 
         grouped = late.tile([P, S, PACK], BF16, name="grouped", offset=0, align_bytes=64)
         late_a = late.tile([P, 2, HALF], F32, name="late_a", offset=GROUPED_BYTES, align_bytes=64)
-        late_b = late.tile([P, 2, P], F32, name="late_b", offset=GROUPED_BYTES + LATE_A_BYTES, align_bytes=64)
 
         def pair_up(j, a, b, src):
             nc.scalar.copy(grouped[:, a:b, j : j + 2], src.rearrange("p j c -> p c j"))
@@ -95,24 +92,22 @@ def tile_picked_gatv_none_e_kernel(tc, xT, w1_words, w1_scales, score, offs, pos
             gather(early[:, 1, a : a + HALF], 1, a, a + HALF)
             pair_up(0, a, a + HALF, early[:, :, a : a + HALF])
         gather(late_a[:, 0, :], 2, 0, HALF)
-        gather(late_b[:, 0, :], 2, HALF, DIRECT)
-        gather(grouped[:, DIRECT:S, 2], 2, DIRECT, S)
+        gather(grouped[:, HALF:S, 2], 2, HALF, S)
         for a in (0, P):
             gather(late_a[:, 1, a : a + P], 3, a, a + P)
             pair_up(2, a, a + P, late_a[:, :, a : a + P])
-        gather(late_b[:, 1, :], 3, HALF, DIRECT)
-        pair_up(2, HALF, DIRECT, late_b[:])
-        gather(grouped[:, DIRECT:S, 3], 3, DIRECT, S)
+        for a in (HALF, HALF + P):
+            gather(grouped[:, a : a + P, 3], 3, a, a + P)
 
         x_scales = keep.tile([P, S], U8, name="x_scales", align_bytes=64)
         y = keep.tile([P, S], F32, name="y")
         codes = {
             0: keep.tile([P, P], U32, name="codes0", align_bytes=64),
             P: keep.tile([P, P], U32, name="codes1", align_bytes=64),
-            HALF: keep.tile([P, P], U32, name="codes2", tag="slot_c", align_bytes=64),
-            DIRECT: late.tile([P, P], U32, name="codes3", offset=GROUPED_BYTES, align_bytes=64),
+            HALF: keep.tile([P, P], U32, name="codes2", align_bytes=64),
+            HALF + P: late.tile([P, P], U32, name="codes3", offset=GROUPED_BYTES, align_bytes=64),
         }
-        order = (0, P, DIRECT, HALF)
+        order = (0, HALF, P, HALF + P)
         for a in order:
             nc.vector.quantize_mx(
                 out=codes[a][:].bitcast(FP8X4),
@@ -135,7 +130,7 @@ def tile_picked_gatv_none_e_kernel(tc, xT, w1_words, w1_scales, score, offs, pos
             else:
                 nc.scalar.copy(y[:, a : a + P], acc[:])
 
-        weights = keep.tile([P, D, P], F32, name="weights", tag="slot_c", align_bytes=64)
+        weights = late.tile([P, D, P], F32, name="weights", offset=GROUPED_BYTES, align_bytes=64)
         nc.scalar.copy(weights[:], spread[:])
         fetched = keep.tile([P, D, P], F32, name="fetched")
         turned = keep.tile([P, D, P], F32, name="turned")

@@ -17,7 +17,7 @@ P = 128
 K, T, S, D, V, N = 512, 1024, 512, 4, 256, 128
 PACK = 4
 HALF = S // 2
-GROUPED_BYTES = S * PACK * 2
+PAIR_BYTES = S * PACK * 2
 ROW_STEP = 129
 ROW0 = 120
 
@@ -33,15 +33,14 @@ def tile_picked_gatv_none_e_kernel(tc, xT, w1_words, w1_scales, score, offs, pos
         late = ctx.enter_context(tc.tile_pool(name="late", bufs=1))
         psum = ctx.enter_context(tc.psum_pool(name="psum", bufs=1))
 
-        early = keep.tile([P, 2, S], F32, name="early")
-        score_rows = early[:, 0, 0:P]
+        score_rows = late.tile([P, P], F32, name="score_rows", offset=PAIR_BYTES, align_bytes=64)
         nc.scalar.dma_start(out=score_rows[ROW0:P, :], in_=score.rearrange("d p (h c) -> (d p h) c", c=P)[0 : D * P * 2 : ROW_STEP, :])
         nc.vector.memset(score_rows[0:ROW0, :], 0.0)
         x_planes = xT.rearrange("(p j) t -> j p t", j=PACK)
         planes = [keep.tile([P, T], F32, name="plane%d" % j) for j in range(PACK)]
         picks = lists.tile([P, S // 16], U16, name="picks")
         nc.sync.dma_start(picks[:], offs)
-        for j in range(PACK):
+        for j in (2, 0, 1, 3):
             nc.sync.dma_start(out=planes[j][:], in_=x_planes[j])
         w_codes = keep.tile([P, N], U32, name="w_codes", align_bytes=64)
         nc.sync.dma_start(out=w_codes[:].bitcast(I32), in_=w1_words[0].rearrange("p n t -> p (n t)").bitcast(I32))
@@ -59,60 +58,69 @@ def tile_picked_gatv_none_e_kernel(tc, xT, w1_words, w1_scales, score, offs, pos
         make_identity(nc, ident[:])
 
         score_bank = psum.tile([P, P], F32, name="score_bank", tag="bank_a")
-        nc.tensor.transpose(score_bank[:], score_rows, ident[:])
+        nc.tensor.transpose(score_bank[:], score_rows[:], ident[:])
         scores = score_bank[:, ROW0:P].rearrange("p (d r) -> p r d", r=2)
-        minus_largest = early[:, 1, 0:2]
-        sums = early[:, 1, HALF : HALF + 2]
+        largest_room = late.tile([P, S + 32], F32, name="largest_room", offset=PAIR_BYTES + PAIR_BYTES // 2 - 64, align_bytes=64)
+        minus_largest = largest_room[:, 0:2]
+        sums = keep.tile([P, 2], F32, name="sums")
         nc.vector.tensor_reduce(minus_largest, scores, mybir.AxisListType.X, ALU.max, negate=True)
-        exps_room = late.tile([P, 128 // 4], F32, name="exps_room", offset=GROUPED_BYTES - 64, align_bytes=64)
-        exps = exps_room[:, 0 : 2 * D].rearrange("p (h d) -> p h d", h=2)
+        exps = keep.tile([P, 2, D], F32, name="exps")
         for h in range(2):
             nc.scalar.activation(exps[:, h, :], scores[:, h, :], ACT.Exp, bias=minus_largest[:, h : h + 1], accum_out=sums[:, h : h + 1])
+
+        pairs = [late.tile([P, 2, HALF, 2], BF16, name="pairs%d" % h, offset=PAIR_BYTES + h * PAIR_BYTES // 2, align_bytes=64) for h in range(2)]
+        spread_room = late.tile([P, S * PACK // 2], F32, name="spread_room", offset=0, align_bytes=64)
+        grouped = [late.tile([P, P, PACK], BF16, name="grouped%d" % i, offset=i * P * PACK * 2, align_bytes=64) for i in range(S // P)]
+        last = S - P
 
         def gather(dst, j, a, b):
             nc.vector.tensor_copy(dst, planes[j][:].indirect(picks[:, a // 16 : b // 16]))
 
-        gather(early[:, 0, :], 0, 0, S)
+        def pair_slot(j, a, b):
+            return pairs[a // HALF][:, j // 2, a % HALF : a % HALF + b - a, j % 2]
+
+        def weave(a):
+            words = pairs[a // HALF][:].rearrange("p u s e -> p u (s e)").bitcast(U32)
+            dst = grouped[a // P][:].rearrange("p s (u e) -> p s u e", e=2).rearrange("p s u e -> p (s u e)").bitcast(U32)
+            nc.scalar.copy(dst.rearrange("p (s u) -> p s u", u=2), words[:, :, a % HALF : a % HALF + P].rearrange("p u s -> p s u"))
+
+        nc.gpsimd.memset(pairs[1][:, 1, P:HALF, :], 0.0)
+        rounded = late.tile([P, T], BF16, name="rounded", offset=2 * PAIR_BYTES, align_bytes=64)
+        nc.scalar.copy(rounded[:], planes[2][:])
+        nc.scalar.activation(pair_slot(2, last, S), rounded[:].indirect(picks[:, last // 16 : S // 16]), ACT.Copy)
+        for a, b in ((0, HALF), (HALF, last)):
+            gather(pair_slot(2, a, b), 2, a, b)
         inv_sums = keep.tile([P, 2], F32, name="inv_sums")
-        nc.vector.reciprocal(inv_sums[:], sums)
-        shares = keep.tile([P, 2, D], F32, name="shares")
-        for h in range(2):
-            nc.scalar.activation(shares[:, h, :], exps[:, h, :], ACT.Copy, scale=inv_sums[:, h : h + 1])
+        nc.vector.reciprocal(inv_sums[:], sums[:])
+        own_shares = keep.tile([P, D], F32, name="own_shares")
+        shares = (own_shares[:], spread_room[:, 0:D])
+        for h in (1, 0):
+            nc.scalar.activation(shares[h], exps[:, h, :], ACT.Copy, scale=inv_sums[:, h : h + 1])
         spread = psum.tile([P, D, P], F32, name="spread", tag="bank_b")
         for d in range(D):
-            nc.tensor.transpose(spread[:, d, :], shares[:, 1, d : d + 1].to_broadcast([P, P]), ident[:])
+            nc.tensor.transpose(spread[:, d, :], shares[1][:, d : d + 1].to_broadcast([P, P]), ident[:])
+        weights = keep.tile([P, D, P], F32, name="weights")
+        nc.scalar.copy(weights[:], spread[:])
 
-        grouped = late.tile([P, S, PACK], BF16, name="grouped", offset=0, align_bytes=64)
-        late_a = late.tile([P, 2, HALF], F32, name="late_a", offset=GROUPED_BYTES, align_bytes=64)
-
-        def pair_up(j, a, b, src):
-            nc.scalar.copy(grouped[:, a:b, j : j + 2], src.rearrange("p j c -> p c j"))
-
-        for a in (0, HALF):
-            gather(early[:, 1, a : a + HALF], 1, a, a + HALF)
-            pair_up(0, a, a + HALF, early[:, :, a : a + HALF])
-        gather(late_a[:, 0, :], 2, 0, HALF)
-        gather(grouped[:, HALF:S, 2], 2, HALF, S)
-        for a in (0, P):
-            gather(late_a[:, 1, a : a + P], 3, a, a + P)
-            pair_up(2, a, a + P, late_a[:, :, a : a + P])
-        for a in (HALF, HALF + P):
-            gather(grouped[:, a : a + P, 3], 3, a, a + P)
+        for j in range(2):
+            for a in (0, HALF):
+                gather(pair_slot(j, a, a + HALF), j, a, a + HALF)
+        weave(last)
+        for a in range(0, last, P):
+            gather(pair_slot(3, a, a + P), 3, a, a + P)
+            weave(a)
+        gather(grouped[last // P][:, :, 3], 3, last, S)
 
         x_scales = keep.tile([P, S], U8, name="x_scales", align_bytes=64)
         y = keep.tile([P, S], F32, name="y")
-        codes = {
-            0: keep.tile([P, P], U32, name="codes0", align_bytes=64),
-            P: keep.tile([P, P], U32, name="codes1", align_bytes=64),
-            HALF: keep.tile([P, P], U32, name="codes2", align_bytes=64),
-            HALF + P: late.tile([P, P], U32, name="codes3", offset=GROUPED_BYTES, align_bytes=64),
-        }
-        order = (0, HALF, P, HALF + P)
+        codes = {a: keep.tile([P, P], U32, name="codes%d" % a, align_bytes=64)[:] for a in range(0, last, P)}
+        codes[last] = late.tile([P, P], U32, name="codes_last", offset=PAIR_BYTES, align_bytes=64)[:]
+        order = (0, P, last, HALF)
         for a in order:
             nc.vector.quantize_mx(
-                out=codes[a][:].bitcast(FP8X4),
+                out=codes[a].bitcast(FP8X4),
                 scales=x_scales[:, a : a + P],
-                in_=grouped[:, a : a + P, :].rearrange("p c j -> p (c j)"),
+                in_=grouped[a // P][:].rearrange("p c j -> p (c j)"),
             )
         for a in order:
             acc = psum.tile([P, P], F32, name="acc%d" % a)
@@ -120,7 +128,7 @@ def tile_picked_gatv_none_e_kernel(tc, xT, w1_words, w1_scales, score, offs, pos
                 out=acc[:],
                 lhsT=w_codes[:].bitcast(FP8X4),
                 lhsT_scale=w_scales[:],
-                rhs=codes[a][:].bitcast(FP8X4),
+                rhs=codes[a].bitcast(FP8X4),
                 rhs_scale=x_scales[:, a : a + P],
                 start=True,
                 stop=True,
@@ -130,8 +138,6 @@ def tile_picked_gatv_none_e_kernel(tc, xT, w1_words, w1_scales, score, offs, pos
             else:
                 nc.scalar.copy(y[:, a : a + P], acc[:])
 
-        weights = late.tile([P, D, P], F32, name="weights", offset=GROUPED_BYTES, align_bytes=64)
-        nc.scalar.copy(weights[:], spread[:])
         fetched = keep.tile([P, D, P], F32, name="fetched")
         turned = keep.tile([P, D, P], F32, name="turned")
         terms = keep.tile([P, D, P], F32, name="terms")
@@ -145,7 +151,7 @@ def tile_picked_gatv_none_e_kernel(tc, xT, w1_words, w1_scales, score, offs, pos
             nc.vector.tensor_copy(fetched[:, d, :], y[:].indirect(places[d][:, 0:cols]))
             forth = psum.tile([P, P], F32, name="forth%d" % d, tag=("bank_a", "acc0", "acc128", "bank_b")[d])
             nc.tensor.transpose(forth[:], fetched[:, d, :], ident[:])
-            nc.scalar.activation(turned[:, d, :], forth[:], ACT.Copy, scale=shares[:, 0, d : d + 1])
+            nc.scalar.activation(turned[:, d, :], forth[:], ACT.Copy, scale=shares[0][:, d : d + 1])
         for d in range(D):
             nc.tensor.matmul(back[:], lhsT=turned[:, d, :], rhs=ident[:], start=(d == 0), stop=(d == D - 1), is_transpose=True)
         nc.scalar.copy(result[:, 0:P], back[:])

@@ -92,15 +92,15 @@ def tile_picked_gatv_none_e_kernel(tc, xT, w1_words, w1_scales, score, offs, pos
             gather(pair_slot(2, a, b), 2, a, b)
         inv_sums = keep.tile([P, 2], F32, name="inv_sums")
         nc.vector.reciprocal(inv_sums[:], sums[:])
-        own_shares = keep.tile([P, D], F32, name="own_shares")
-        shares = (own_shares[:], spread_room[:, 0:D])
-        for h in (1, 0):
-            nc.scalar.activation(shares[h], exps[:, h, :], ACT.Copy, scale=inv_sums[:, h : h + 1])
-        spread = psum.tile([P, D, P], F32, name="spread", tag="bank_b")
+        shares = spread_room[:, 0 : 2 * D].rearrange("p (h d) -> p h d", d=D)
+        for h in range(2):
+            nc.scalar.activation(shares[:, h, :], exps[:, h, :], ACT.Copy, scale=inv_sums[:, h : h + 1])
+        spread = [psum.tile([P, 2, V], F32, name="spread%d" % b) for b in range(2)]
         for d in range(D):
-            nc.tensor.transpose(spread[:, d, :], shares[1][:, d : d + 1].to_broadcast([P, P]), ident[:])
-        weights = keep.tile([P, D, P], F32, name="weights")
-        nc.scalar.copy(weights[:], spread[:])
+            for h in range(2):
+                nc.tensor.transpose(spread[d // 2][:, d % 2, h * P : (h + 1) * P], shares[:, h, d : d + 1].to_broadcast([P, P]), ident[:])
+        weights0 = keep.tile([P, V], F32, name="weights0")
+        nc.scalar.copy(weights0[:], spread[0][:, 0, :])
 
         for j in range(2):
             for a in (0, HALF):
@@ -138,34 +138,29 @@ def tile_picked_gatv_none_e_kernel(tc, xT, w1_words, w1_scales, score, offs, pos
             else:
                 nc.scalar.copy(y[:, a : a + P], acc[:])
 
-        fetched = keep.tile([P, D, P], F32, name="fetched")
-        turned = keep.tile([P, D, P], F32, name="turned")
-        terms = keep.tile([P, D, P], F32, name="terms")
-        sum01 = keep.tile([P, P], F32, name="sum01")
-        sum012 = keep.tile([P, P], F32, name="sum012")
-        result = keep.tile([P, V], F32, name="result")
         cols = P // 16
+        fetched = [[keep.tile([P, P], F32, name="fetched%d_%d" % (d, h)) for h in range(2)] for d in range(1, D)]
+        terms = [[keep.tile([P, P], F32, name="terms%d_%d" % (d, h)) for h in range(2)] for d in range(1, D)]
+        first = keep.tile([P, V], F32, name="first")
+        for d in range(1, D):
+            for h in range(2):
+                nc.scalar.activation(fetched[d - 1][h][:], y[:].indirect(places[d][:, h * cols : (h + 1) * cols]), ACT.Copy)
+        nc.vector.tensor_tensor(first[:], y[:].indirect(places[0][:]), weights0[:], ALU.mult)
+        partial = [first[:, 0:P], first[:, P:V]]
 
-        back = psum.tile([P, P], F32, name="back")
-        for d in range(D):
-            nc.vector.tensor_copy(fetched[:, d, :], y[:].indirect(places[d][:, 0:cols]))
-            forth = psum.tile([P, P], F32, name="forth%d" % d, tag=("bank_a", "acc0", "acc128", "bank_b")[d])
-            nc.tensor.transpose(forth[:], fetched[:, d, :], ident[:])
-            nc.scalar.activation(turned[:, d, :], forth[:], ACT.Copy, scale=shares[0][:, d : d + 1])
-        for d in range(D):
-            nc.tensor.matmul(back[:], lhsT=turned[:, d, :], rhs=ident[:], start=(d == 0), stop=(d == D - 1), is_transpose=True)
-        nc.scalar.copy(result[:, 0:P], back[:])
-        nc.scalar.dma_start(out=out[:, 0:P], in_=result[:, 0:P])
+        def weigh(d, h):
+            nc.vector.tensor_tensor(terms[d - 1][h][:], fetched[d - 1][h][:], spread[d // 2][:, d % 2, h * P : (h + 1) * P], ALU.mult)
 
-        def weigh(d):
-            nc.vector.tensor_tensor(terms[:, d, :], y[:].indirect(places[d][:, cols : 2 * cols]), weights[:, d, :], ALU.mult)
+        def add(d, h):
+            total = keep.tile([P, P], F32, name="total%d_%d" % (d, h))
+            nc.vector.tensor_tensor(total[:], partial[h], terms[d - 1][h][:], ALU.add)
+            partial[h] = total[:]
 
-        for d in range(3):
-            weigh(d)
-        nc.vector.tensor_tensor(sum01[:], terms[:, 0, :], terms[:, 1, :], ALU.add)
-        weigh(3)
-        for c in (0, P // 2):
-            nc.vector.tensor_tensor(sum012[:, c : c + P // 2], sum01[:, c : c + P // 2], terms[:, 2, c : c + P // 2], ALU.add)
-        for c in (0, P // 2):
-            nc.vector.tensor_tensor(result[:, P + c : P + c + P // 2], sum012[:, c : c + P // 2], terms[:, 3, c : c + P // 2], ALU.add)
-        nc.sync.dma_start(out=out[:, P:V], in_=result[:, P:V])
+        steps = [(d, h) for d in range(1, D) for h in range(2)]
+        weigh(*steps[0])
+        for i in range(1, len(steps)):
+            weigh(*steps[i])
+            add(*steps[i - 1])
+        add(*steps[-1])
+        nc.scalar.dma_start(out=out[:, 0:P], in_=partial[0])
+        nc.sync.dma_start(out=out[:, P:V], in_=partial[1])

@@ -18,6 +18,8 @@ K, T, S, D, V, N = 512, 1024, 512, 4, 256, 128
 PACK = 4
 HALF = S // 2
 PAIR_BYTES = S * PACK * 2
+PLANES_AT = 2048
+REUSE_AT = PLANES_AT + 3 * T * 4
 ROW_STEP = 129
 ROW0 = 120
 
@@ -33,14 +35,14 @@ def tile_picked_gatv_none_e_kernel(tc, xT, w1_words, w1_scales, score, offs, pos
         late = ctx.enter_context(tc.tile_pool(name="late", bufs=1))
         psum = ctx.enter_context(tc.psum_pool(name="psum", bufs=1))
 
-        score_rows = late.tile([P, P], F32, name="score_rows", offset=PAIR_BYTES, align_bytes=64)
+        score_rows = keep.tile([P, P], F32, name="score_rows")
         nc.scalar.dma_start(out=score_rows[ROW0:P, :], in_=score.rearrange("d p (h c) -> (d p h) c", c=P)[0 : D * P * 2 : ROW_STEP, :])
         nc.vector.memset(score_rows[0:ROW0, :], 0.0)
         x_planes = xT.rearrange("(p j) t -> j p t", j=PACK)
-        planes = [keep.tile([P, T], F32, name="plane%d" % j) for j in range(PACK)]
+        planes = [late.tile([P, T], F32, name="plane%d" % j, offset=PLANES_AT + (0, 3, 1, 2)[j] * T * 4, align_bytes=64) for j in range(PACK)]
         picks = lists.tile([P, S // 16], U16, name="picks")
         nc.sync.dma_start(picks[:], offs)
-        for j in (2, 0, 1, 3):
+        for j in range(PACK):
             nc.sync.dma_start(out=planes[j][:], in_=x_planes[j])
         w_codes = keep.tile([P, N], U32, name="w_codes", align_bytes=64)
         nc.sync.dma_start(out=w_codes[:].bitcast(I32), in_=w1_words[0].rearrange("p n t -> p (n t)").bitcast(I32))
@@ -60,67 +62,74 @@ def tile_picked_gatv_none_e_kernel(tc, xT, w1_words, w1_scales, score, offs, pos
         score_bank = psum.tile([P, P], F32, name="score_bank", tag="bank_a")
         nc.tensor.transpose(score_bank[:], score_rows[:], ident[:])
         scores = score_bank[:, ROW0:P].rearrange("p (d r) -> p r d", r=2)
-        largest_room = late.tile([P, S + 32], F32, name="largest_room", offset=PAIR_BYTES + PAIR_BYTES // 2 - 64, align_bytes=64)
-        minus_largest = largest_room[:, 0:2]
+        minus_largest = late.tile([P, 2], F32, name="minus_largest", offset=0, align_bytes=64)[:]
         sums = keep.tile([P, 2], F32, name="sums")
         nc.vector.tensor_reduce(minus_largest, scores, mybir.AxisListType.X, ALU.max, negate=True)
         exps = keep.tile([P, 2, D], F32, name="exps")
         for h in range(2):
             nc.scalar.activation(exps[:, h, :], scores[:, h, :], ACT.Exp, bias=minus_largest[:, h : h + 1], accum_out=sums[:, h : h + 1])
 
-        pairs = [late.tile([P, 2, HALF, 2], BF16, name="pairs%d" % h, offset=PAIR_BYTES + h * PAIR_BYTES // 2, align_bytes=64) for h in range(2)]
-        spread_room = late.tile([P, S * PACK // 2], F32, name="spread_room", offset=0, align_bytes=64)
-        grouped = [late.tile([P, P, PACK], BF16, name="grouped%d" % i, offset=i * P * PACK * 2, align_bytes=64) for i in range(S // P)]
-        last = S - P
+        pairs = late.tile([P, 2, HALF, 2], BF16, name="pairs", offset=0, align_bytes=64)
+        flat01 = pairs[:, 1, :, :].rearrange("p s e -> p (s e)").rearrange("p (e s) -> p e s", e=2)
+        slotted = [late.tile([P, P, PACK], BF16, name="slotted%d" % i, offset=REUSE_AT + i * 1024, align_bytes=64) for i in range(2)]
+        flat2 = late.tile([P, P], BF16, name="flat2", offset=REUSE_AT + 2432, align_bytes=64)
+        flat3 = late.tile([P, HALF], BF16, name="flat3", offset=REUSE_AT + 2048, align_bytes=64)
+        woven = late.tile([P, HALF * PACK], BF16, name="woven", offset=REUSE_AT + 2560, align_bytes=64)
 
-        def gather(dst, j, a, b):
-            nc.vector.tensor_copy(dst, planes[j][:].indirect(picks[:, a // 16 : b // 16]))
+        def picked(j, a, b):
+            return planes[j][:].indirect(picks[:, a // 16 : b // 16])
 
-        def pair_slot(j, a, b):
-            return pairs[a // HALF][:, j // 2, a % HALF : a % HALF + b - a, j % 2]
+        def pair_gather(j, a, b):
+            nc.vector.tensor_copy(pairs[:, j // 2, a:b, j % 2], picked(j, a, b))
 
         def weave(a):
-            words = pairs[a // HALF][:].rearrange("p u s e -> p u (s e)").bitcast(U32)
-            dst = grouped[a // P][:].rearrange("p s (u e) -> p s u e", e=2).rearrange("p s u e -> p (s u e)").bitcast(U32)
-            nc.scalar.copy(dst.rearrange("p (s u) -> p s u", u=2), words[:, :, a % HALF : a % HALF + P].rearrange("p u s -> p s u"))
+            words = pairs[:].rearrange("p u s e -> p u (s e)").bitcast(U32)
+            dst = woven[:, a * PACK : (a + P) * PACK].bitcast(U32)
+            nc.scalar.copy(dst.rearrange("p (s u) -> p s u", u=2), words[:, :, a : a + P].rearrange("p u s -> p s u"))
 
-        nc.gpsimd.memset(pairs[1][:, 1, P:HALF, :], 0.0)
-        rounded = late.tile([P, T], BF16, name="rounded", offset=2 * PAIR_BYTES, align_bytes=64)
-        nc.scalar.copy(rounded[:], planes[2][:])
-        nc.scalar.activation(pair_slot(2, last, S), rounded[:].indirect(picks[:, last // 16 : S // 16]), ACT.Copy)
-        for a, b in ((0, HALF), (HALF, last)):
-            gather(pair_slot(2, a, b), 2, a, b)
+        pair_gather(0, 0, HALF)
+        nc.scalar.activation(flat01[:, 0, :], picked(0, HALF, S), ACT.Copy)
         inv_sums = keep.tile([P, 2], F32, name="inv_sums")
         nc.vector.reciprocal(inv_sums[:], sums[:])
-        shares = spread_room[:, 0 : 2 * D].rearrange("p (h d) -> p h d", d=D)
-        for h in range(2):
-            nc.scalar.activation(shares[:, h, :], exps[:, h, :], ACT.Copy, scale=inv_sums[:, h : h + 1])
+        shares = keep.tile([P, 2, D], F32, name="shares")
+        nc.vector.tensor_tensor(shares[:], exps[:], inv_sums[:].unsqueeze(2).to_broadcast([P, 2, D]), ALU.mult)
         spread = [psum.tile([P, 2, V], F32, name="spread%d" % b) for b in range(2)]
         for d in range(D):
             for h in range(2):
                 nc.tensor.transpose(spread[d // 2][:, d % 2, h * P : (h + 1) * P], shares[:, h, d : d + 1].to_broadcast([P, P]), ident[:])
-        weights0 = keep.tile([P, V], F32, name="weights0")
-        nc.scalar.copy(weights0[:], spread[0][:, 0, :])
 
-        for j in range(2):
-            for a in (0, HALF):
-                gather(pair_slot(j, a, a + HALF), j, a, a + HALF)
-        weave(last)
-        for a in range(0, last, P):
-            gather(pair_slot(3, a, a + P), 3, a, a + P)
-            weave(a)
-        gather(grouped[last // P][:, :, 3], 3, last, S)
+        pair_gather(1, 0, HALF)
+        for i in range(2):
+            nc.scalar.activation(flat01[:, 1, i * P : (i + 1) * P], picked(1, HALF + i * P, HALF + (i + 1) * P), ACT.Copy)
+        for i in range(2):
+            nc.vector.tensor_copy(slotted[i][:, :, 0:2], flat01[:, :, i * P : (i + 1) * P].rearrange("p e s -> p s e"))
+        nc.vector.tensor_copy(slotted[0][:, :, 2], picked(2, HALF, HALF + P))
+        pair_gather(2, 0, HALF)
+        nc.scalar.activation(flat2[:], picked(2, HALF + P, S), ACT.Copy)
+        nc.scalar.copy(slotted[1][:, :, 2], flat2[:])
+        for i in range(2):
+            pair_gather(3, i * P, (i + 1) * P)
+        for i in range(2):
+            nc.scalar.activation(flat3[:, i * P : (i + 1) * P], picked(3, HALF + i * P, HALF + (i + 1) * P), ACT.Copy)
+        for i in range(2):
+            nc.vector.tensor_copy(slotted[i][:, :, 3], flat3[:, i * P : (i + 1) * P])
+        for i in range(2):
+            weave(i * P)
+        weights0 = late.tile([P, V], F32, name="weights0", offset=0, align_bytes=64)
+        nc.scalar.copy(weights0[:], spread[0][:, 0, :])
 
         x_scales = keep.tile([P, S], U8, name="x_scales", align_bytes=64)
         y = keep.tile([P, S], F32, name="y")
-        codes = {a: keep.tile([P, P], U32, name="codes%d" % a, align_bytes=64)[:] for a in range(0, last, P)}
-        codes[last] = late.tile([P, P], U32, name="codes_last", offset=PAIR_BYTES, align_bytes=64)[:]
-        order = (0, P, last, HALF)
+        codes = {a: keep.tile([P, P], U32, name="codes%d" % a, align_bytes=64)[:] for a in range(0, S, P)}
+        order = (HALF, 0, HALF + P, P)
+        grouped = {a: woven[:, a * PACK : (a + P) * PACK] for a in (0, P)}
+        for i in range(2):
+            grouped[HALF + i * P] = slotted[i][:].rearrange("p c j -> p (c j)")
         for a in order:
             nc.vector.quantize_mx(
                 out=codes[a].bitcast(FP8X4),
                 scales=x_scales[:, a : a + P],
-                in_=grouped[a // P][:].rearrange("p c j -> p (c j)"),
+                in_=grouped[a],
             )
         for a in order:
             acc = psum.tile([P, P], F32, name="acc%d" % a)

@@ -20,6 +20,7 @@ HALF = S // 2
 PAIR_BYTES = S * PACK * 2
 PLANES_AT = 2048
 REUSE_AT = PLANES_AT + 3 * T * 4
+FUSED = 64
 ROW_STEP = 129
 ROW0 = 120
 
@@ -71,10 +72,10 @@ def tile_picked_gatv_none_e_kernel(tc, xT, w1_words, w1_scales, score, offs, pos
 
         pairs = late.tile([P, 2, HALF, 2], BF16, name="pairs", offset=0, align_bytes=64)
         flat01 = pairs[:, 1, :, :].rearrange("p s e -> p (s e)").rearrange("p (e s) -> p e s", e=2)
-        slotted = [late.tile([P, P, PACK], BF16, name="slotted%d" % i, offset=REUSE_AT + i * 1024, align_bytes=64) for i in range(2)]
-        flat2 = late.tile([P, P], BF16, name="flat2", offset=REUSE_AT + 2432, align_bytes=64)
-        flat3 = late.tile([P, HALF], BF16, name="flat3", offset=REUSE_AT + 2048, align_bytes=64)
-        woven = late.tile([P, HALF * PACK], BF16, name="woven", offset=REUSE_AT + 2560, align_bytes=64)
+        slotted = [late.tile([P, P, PACK], BF16, name="slotted%d" % i, offset=(PLANES_AT, REUSE_AT)[i], align_bytes=64) for i in range(2)]
+        flat2 = [late.tile([P, P // 2], BF16, name="flat2_%d" % i, offset=REUSE_AT + (2624, 2048)[i], align_bytes=64) for i in range(2)]
+        flat3 = late.tile([P, HALF], BF16, name="flat3", offset=REUSE_AT + 2176, align_bytes=64)
+        woven = late.tile([P, HALF * PACK], BF16, name="woven", offset=REUSE_AT + 2688, align_bytes=64)
 
         def picked(j, a, b):
             return planes[j][:].indirect(picks[:, a // 16 : b // 16])
@@ -87,26 +88,33 @@ def tile_picked_gatv_none_e_kernel(tc, xT, w1_words, w1_scales, score, offs, pos
             dst = woven[:, a * PACK : (a + P) * PACK].bitcast(U32)
             nc.scalar.copy(dst.rearrange("p (s u) -> p s u", u=2), words[:, :, a : a + P].rearrange("p u s -> p s u"))
 
-        pair_gather(0, 0, HALF)
-        nc.scalar.activation(flat01[:, 0, :], picked(0, HALF, S), ACT.Copy)
         inv_sums = keep.tile([P, 2], F32, name="inv_sums")
         nc.vector.reciprocal(inv_sums[:], sums[:])
+        pair_gather(0, 0, HALF)
+        nc.scalar.activation(flat01[:, 0, :], picked(0, HALF, S), ACT.Copy)
         shares = keep.tile([P, 2, D], F32, name="shares")
         nc.vector.tensor_tensor(shares[:], exps[:], inv_sums[:].unsqueeze(2).to_broadcast([P, 2, D]), ALU.mult)
         spread = [psum.tile([P, 2, V], F32, name="spread%d" % b) for b in range(2)]
+
+        def share_of(d, a, b):
+            bank, slot = ((0, 1), (1, 0), (1, 1), (0, 0))[d]
+            return spread[bank][:, slot, a:b]
+
         for d in range(D):
             for h in range(2):
-                nc.tensor.transpose(spread[d // 2][:, d % 2, h * P : (h + 1) * P], shares[:, h, d : d + 1].to_broadcast([P, P]), ident[:])
+                nc.tensor.transpose(share_of(d, h * P, (h + 1) * P), shares[:, h, d : d + 1].to_broadcast([P, P]), ident[:])
 
         pair_gather(1, 0, HALF)
         for i in range(2):
             nc.scalar.activation(flat01[:, 1, i * P : (i + 1) * P], picked(1, HALF + i * P, HALF + (i + 1) * P), ACT.Copy)
         for i in range(2):
             nc.vector.tensor_copy(slotted[i][:, :, 0:2], flat01[:, :, i * P : (i + 1) * P].rearrange("p e s -> p s e"))
-        nc.vector.tensor_copy(slotted[0][:, :, 2], picked(2, HALF, HALF + P))
+        nc.vector.tensor_copy(slotted[1][:, :, 2], picked(2, HALF + P, S))
         pair_gather(2, 0, HALF)
-        nc.scalar.activation(flat2[:], picked(2, HALF + P, S), ACT.Copy)
-        nc.scalar.copy(slotted[1][:, :, 2], flat2[:])
+        for i, a in enumerate((0, P // 2)):
+            nc.scalar.activation(flat2[i][:], picked(2, HALF + a, HALF + a + P // 2), ACT.Copy)
+        for i, a in enumerate((0, P // 2)):
+            nc.scalar.copy(slotted[0][:, a : a + P // 2, 2], flat2[i][:])
         for i in range(2):
             pair_gather(3, i * P, (i + 1) * P)
         for i in range(2):
@@ -115,12 +123,13 @@ def tile_picked_gatv_none_e_kernel(tc, xT, w1_words, w1_scales, score, offs, pos
             nc.vector.tensor_copy(slotted[i][:, :, 3], flat3[:, i * P : (i + 1) * P])
         for i in range(2):
             weave(i * P)
-        weights0 = late.tile([P, V], F32, name="weights0", offset=0, align_bytes=64)
-        nc.scalar.copy(weights0[:], spread[0][:, 0, :])
+        weights = late.tile([P, FUSED + V], F32, name="weights", offset=0, align_bytes=64)
+        nc.scalar.copy(weights[:], spread[0][:].rearrange("p d v -> p (d v)")[:, V - FUSED : 2 * V])
 
         x_scales = keep.tile([P, S], U8, name="x_scales", align_bytes=64)
         y = keep.tile([P, S], F32, name="y")
-        codes = {a: keep.tile([P, P], U32, name="codes%d" % a, align_bytes=64)[:] for a in range(0, S, P)}
+        codes = {a: keep.tile([P, P], U32, name="codes%d" % a, align_bytes=64)[:] for a in (0, P, HALF + P)}
+        codes[HALF] = late.tile([P, P], U32, name="codes_first", offset=PLANES_AT + 2 * T * 4, align_bytes=64)[:]
         order = (HALF, 0, HALF + P, P)
         grouped = {a: woven[:, a * PACK : (a + P) * PACK] for a in (0, P)}
         for i in range(2):
@@ -147,29 +156,38 @@ def tile_picked_gatv_none_e_kernel(tc, xT, w1_words, w1_scales, score, offs, pos
             else:
                 nc.scalar.copy(y[:, a : a + P], acc[:])
 
-        cols = P // 16
-        fetched = [[keep.tile([P, P], F32, name="fetched%d_%d" % (d, h)) for h in range(2)] for d in range(1, D)]
-        terms = [[keep.tile([P, P], F32, name="terms%d_%d" % (d, h)) for h in range(2)] for d in range(1, D)]
-        first = keep.tile([P, V], F32, name="first")
+        def looked_up(d, a, b):
+            return y[:].indirect(places[d][:, a // 16 : b // 16])
+
+        cut = V - FUSED
+        fetched = [None] + [keep.tile([P, V], F32, name="fetched%d" % d) for d in range(1, D)]
+        terms = [keep.tile([P, V], F32, name="terms%d" % d) for d in range(D)]
+        totals = [keep.tile([P, V], F32, name="totals%d" % d) for d in range(2)]
         for d in range(1, D):
-            for h in range(2):
-                nc.scalar.activation(fetched[d - 1][h][:], y[:].indirect(places[d][:, h * cols : (h + 1) * cols]), ACT.Copy)
-        nc.vector.tensor_tensor(first[:], y[:].indirect(places[0][:]), weights0[:], ALU.mult)
-        partial = [first[:, 0:P], first[:, P:V]]
+            for a, b in ((0, P), (P, V if d < D - 1 else cut)):
+                nc.scalar.activation(fetched[d][:, a:b], looked_up(d, a, b), ACT.Copy)
+        nc.vector.tensor_tensor(terms[0][:], looked_up(0, 0, V), weights[:, FUSED:], ALU.mult)
+        nc.vector.tensor_tensor(terms[3][:, cut:V], looked_up(3, cut, V), weights[:, 0:FUSED], ALU.mult)
 
-        def weigh(d, h):
-            nc.vector.tensor_tensor(terms[d - 1][h][:], fetched[d - 1][h][:], spread[d // 2][:, d % 2, h * P : (h + 1) * P], ALU.mult)
+        def weigh(d, a, b):
+            nc.vector.tensor_tensor(terms[d][:, a:b], fetched[d][:, a:b], share_of(d, a, b), ALU.mult)
 
-        def add(d, h):
-            total = keep.tile([P, P], F32, name="total%d_%d" % (d, h))
-            nc.vector.tensor_tensor(total[:], partial[h], terms[d - 1][h][:], ALU.add)
-            partial[h] = total[:]
+        def add(dst, src, d, a, b):
+            nc.vector.tensor_tensor(dst[:, a:b], src[:, a:b], terms[d][:, a:b], ALU.add)
 
-        steps = [(d, h) for d in range(1, D) for h in range(2)]
-        weigh(*steps[0])
-        for i in range(1, len(steps)):
-            weigh(*steps[i])
-            add(*steps[i - 1])
-        add(*steps[-1])
-        nc.scalar.dma_start(out=out[:, 0:P], in_=partial[0])
-        nc.sync.dma_start(out=out[:, P:V], in_=partial[1])
+        weigh(1, 0, P)
+        weigh(1, P, V)
+        add(terms[0], terms[0], 3, cut, V)
+        add(totals[0], terms[0], 1, 0, P)
+        weigh(2, 0, P)
+        add(totals[0], terms[0], 1, P, V)
+        weigh(2, P, V)
+        add(totals[1], totals[0], 2, 0, P)
+        weigh(3, 0, P)
+        add(totals[1], totals[0], 2, P, cut)
+        weigh(3, P, cut)
+        add(totals[1], totals[0], 2, cut, V)
+        add(totals[1], totals[1], 3, 0, P)
+        add(totals[1], totals[1], 3, P, cut)
+        nc.scalar.dma_start(out=out[:, 0:P], in_=totals[1][:, 0:P])
+        nc.sync.dma_start(out=out[:, P:V], in_=totals[1][:, P:V])

@@ -83,10 +83,10 @@ def tile_picked_gatv_none_e_kernel(tc, xT, w1_words, w1_scales, score, offs, pos
         def pair_gather(j, a, b):
             nc.vector.tensor_copy(pairs[:, j // 2, a:b, j % 2], picked(j, a, b))
 
-        def weave(a):
-            words = pairs[:].rearrange("p u s e -> p u (s e)").bitcast(U32)
-            dst = woven[:, a * PACK : (a + P) * PACK].bitcast(U32)
-            nc.scalar.copy(dst.rearrange("p (s u) -> p s u", u=2), words[:, :, a : a + P].rearrange("p u s -> p s u"))
+        def weave(copy, word, a, b):
+            words = pairs[:].rearrange("p u s e -> p u (s e)").bitcast(word)[:, :, a:b]
+            dst = woven[:, a * PACK : b * PACK].bitcast(word)
+            copy(dst.rearrange("p (s u) -> p s u", u=2), words.rearrange("p u s -> p s u"))
 
         inv_sums = keep.tile([P, 2], F32, name="inv_sums")
         nc.vector.reciprocal(inv_sums[:], sums[:])
@@ -117,12 +117,13 @@ def tile_picked_gatv_none_e_kernel(tc, xT, w1_words, w1_scales, score, offs, pos
             nc.scalar.copy(slotted[0][:, a : a + P // 2, 2], flat2[i][:])
         for i in range(2):
             pair_gather(3, i * P, (i + 1) * P)
+        weave(nc.vector.tensor_copy, I32, 0, P // 2)
         for i in range(2):
             nc.scalar.activation(flat3[:, i * P : (i + 1) * P], picked(3, HALF + i * P, HALF + (i + 1) * P), ACT.Copy)
         for i in range(2):
             nc.vector.tensor_copy(slotted[i][:, :, 3], flat3[:, i * P : (i + 1) * P])
-        for i in range(2):
-            weave(i * P)
+        weave(nc.scalar.copy, U32, P // 2, P)
+        weave(nc.scalar.copy, U32, P, HALF)
         weights = late.tile([P, FUSED + V], F32, name="weights", offset=0, align_bytes=64)
         nc.scalar.copy(weights[:], spread[0][:].rearrange("p d v -> p (d v)")[:, V - FUSED : 2 * V])
 
@@ -189,5 +190,6 @@ def tile_picked_gatv_none_e_kernel(tc, xT, w1_words, w1_scales, score, offs, pos
         add(totals[1], totals[0], 2, cut, V)
         add(totals[1], totals[1], 3, 0, P)
         add(totals[1], totals[1], 3, P, cut)
+        nc.scalar.dma_start(out=out[:, cut:V], in_=totals[1][:, cut:V])
         nc.scalar.dma_start(out=out[:, 0:P], in_=totals[1][:, 0:P])
-        nc.sync.dma_start(out=out[:, P:V], in_=totals[1][:, P:V])
+        nc.sync.dma_start(out=out[:, P:cut], in_=totals[1][:, P:cut])

@@ -42,9 +42,10 @@ def tile_picked_gatv_none_e_kernel(tc, xT, w1_words, w1_scales, score, offs, pos
         x_planes = xT.rearrange("(p j) t -> j p t", j=PACK)
         planes = [late.tile([P, T], F32, name="plane%d" % j, offset=PLANES_AT + (0, 3, 1, 2)[j] * T * 4, align_bytes=64) for j in range(PACK)]
         picks = lists.tile([P, S // 16], U16, name="picks")
-        nc.sync.dma_start(picks[:], offs)
         for j in range(PACK):
             nc.sync.dma_start(out=planes[j][:], in_=x_planes[j])
+            if j == 0:
+                nc.sync.dma_start(picks[:], offs)
         w_codes = keep.tile([P, N], U32, name="w_codes", align_bytes=64)
         nc.sync.dma_start(out=w_codes[:].bitcast(I32), in_=w1_words[0].rearrange("p n t -> p (n t)").bitcast(I32))
         w_scales = keep.tile([P, N], U8, name="w_scales", align_bytes=64)

@@ -16,13 +16,19 @@ ACT = mybir.ActivationFunctionType
 P = 128
 K, T, S, D, V, N = 512, 1024, 512, 4, 256, 128
 PACK = 4
-HALF = S // 2
-PAIR_BYTES = S * PACK * 2
-PLANES_AT = 2048
-REUSE_AT = PLANES_AT + 3 * T * 4
+PAIRED = S // 2
+PER_COLUMN = 16
+SHORT = P // 2
 FUSED = 64
-ROW_STEP = 129
-ROW0 = 120
+SCORE_ROWS = 2 * D
+FIRST_SCORE_ROW = P - SCORE_ROWS
+
+PIECE_BYTES = P * PACK * 2
+PLANE_BYTES = T * 4
+PLANE_AT = [2 * PIECE_BYTES + place * PLANE_BYTES for place in (0, 3, 1, 2)]
+SHORT_BYTES = SHORT * 2
+FLAT_AT = PLANE_AT[1] + 2 * PIECE_BYTES
+WOVEN_AT = FLAT_AT + SHORT_BYTES + PAIRED * 2
 
 FLOPS = 2 * K * S * N
 BYTES = 4 * K * T + K * N + K * N // 32 + 4 * D * V + 2 * (S + D * V) + 4 * N * V
@@ -33,56 +39,67 @@ def tile_picked_gatv_none_e_kernel(tc, xT, w1_words, w1_scales, score, offs, pos
     with ExitStack() as ctx:
         lists = ctx.enter_context(tc.tile_pool(name="lists", bufs=1))
         keep = ctx.enter_context(tc.tile_pool(name="keep", bufs=1))
-        late = ctx.enter_context(tc.tile_pool(name="late", bufs=1))
+        placed = ctx.enter_context(tc.tile_pool(name="placed", bufs=1))
         psum = ctx.enter_context(tc.psum_pool(name="psum", bufs=1))
 
         score_rows = keep.tile([P, P], F32, name="score_rows")
-        nc.scalar.dma_start(out=score_rows[ROW0:P, :], in_=score.rearrange("d p (h c) -> (d p h) c", c=P)[0 : D * P * 2 : ROW_STEP, :])
-        nc.vector.memset(score_rows[0:ROW0, :], 0.0)
+        half_rows = score.rearrange("d p (h c) -> (d p h) c", c=P)
+        nc.scalar.dma_start(out=score_rows[FIRST_SCORE_ROW:P, :], in_=half_rows[0 : D * P * 2 : P + 1, :])
+        nc.vector.memset(score_rows[0:FIRST_SCORE_ROW, :], 0.0)
         x_planes = xT.rearrange("(p j) t -> j p t", j=PACK)
-        planes = [late.tile([P, T], F32, name="plane%d" % j, offset=PLANES_AT + (0, 3, 1, 2)[j] * T * 4, align_bytes=64) for j in range(PACK)]
-        picks = lists.tile([P, S // 16], U16, name="picks")
-        for j in range(PACK):
+        planes = [placed.tile([P, T], F32, name="plane%d" % j, offset=PLANE_AT[j], align_bytes=64) for j in range(PACK)]
+        picks = lists.tile([P, S // PER_COLUMN], U16, name="picks")
+        nc.sync.dma_start(out=planes[0][:], in_=x_planes[0])
+        nc.sync.dma_start(picks[:], offs)
+        for j in range(1, PACK):
             nc.sync.dma_start(out=planes[j][:], in_=x_planes[j])
-            if j == 0:
-                nc.sync.dma_start(picks[:], offs)
         w_codes = keep.tile([P, N], U32, name="w_codes", align_bytes=64)
         nc.sync.dma_start(out=w_codes[:].bitcast(I32), in_=w1_words[0].rearrange("p n t -> p (n t)").bitcast(I32))
         w_scales = keep.tile([P, N], U8, name="w_scales", align_bytes=64)
         nc.vector.memset(w_scales[:].bitcast(I32), 0)
-        for q in range(4):
-            nc.sync.dma_start(out=w_scales[32 * q : 32 * q + 4, :].bitcast(I32), in_=w1_scales[0, 4 * q : 4 * q + 4, :].bitcast(I32))
+
+        def load_scale_rows(queue, q):
+            queue.dma_start(out=w_scales[32 * q : 32 * q + 4, :].bitcast(I32), in_=w1_scales[0, 4 * q : 4 * q + 4, :].bitcast(I32))
+
+        for q in (0, 1):
+            load_scale_rows(nc.sync, q)
         places = []
         for d, pos in enumerate((pos1, pos2, pos3, pos4)):
-            place = lists.tile([P, V // 16], U16, name="place%d" % d)
+            place = lists.tile([P, V // PER_COLUMN], U16, name="place%d" % d)
             nc.sync.dma_start(place[:], pos)
             places.append(place)
 
         ident = keep.tile([P, P], F32, name="ident")
         make_identity(nc, ident[:])
+        for q in (2, 3):
+            load_scale_rows(nc.gpsimd, q)
 
-        score_bank = psum.tile([P, P], F32, name="score_bank", tag="bank_a")
+        score_bank = psum.tile([P, P], F32, name="score_bank")
         nc.tensor.transpose(score_bank[:], score_rows[:], ident[:])
-        scores = score_bank[:, ROW0:P].rearrange("p (d r) -> p r d", r=2)
-        minus_largest = late.tile([P, 2], F32, name="minus_largest", offset=0, align_bytes=64)[:]
+        scores = score_bank[:, FIRST_SCORE_ROW:P].rearrange("p (d h) -> p h d", h=2)
+        minus_largest = placed.tile([P, 2], F32, name="minus_largest", offset=0, align_bytes=64)
         sums = keep.tile([P, 2], F32, name="sums")
-        nc.vector.tensor_reduce(minus_largest, scores, mybir.AxisListType.X, ALU.max, negate=True)
+        nc.vector.tensor_reduce(minus_largest[:], scores, mybir.AxisListType.X, ALU.max, negate=True)
         exps = keep.tile([P, 2, D], F32, name="exps")
         for h in range(2):
             nc.scalar.activation(exps[:, h, :], scores[:, h, :], ACT.Exp, bias=minus_largest[:, h : h + 1], accum_out=sums[:, h : h + 1])
 
-        pairs = late.tile([P, 2, HALF, 2], BF16, name="pairs", offset=0, align_bytes=64)
-        flat01 = pairs[:, 1, :, :].rearrange("p s e -> p (s e)").rearrange("p (e s) -> p e s", e=2)
-        slotted = [late.tile([P, P, PACK], BF16, name="slotted%d" % i, offset=(PLANES_AT, REUSE_AT)[i], align_bytes=64) for i in range(2)]
-        flat2 = [late.tile([P, P // 2], BF16, name="flat2_%d" % i, offset=REUSE_AT + (2624, 2048)[i], align_bytes=64) for i in range(2)]
-        flat3 = late.tile([P, HALF], BF16, name="flat3", offset=REUSE_AT + 2176, align_bytes=64)
-        woven = late.tile([P, HALF * PACK], BF16, name="woven", offset=REUSE_AT + 2688, align_bytes=64)
+        pairs = placed.tile([P, 2, PAIRED, 2], BF16, name="pairs", offset=0, align_bytes=64)
+        flat01 = pairs[:, 1, :, :].rearrange("p s e -> p (s e)").rearrange("p (j s) -> p j s", j=2)
+        slotted = [placed.tile([P, P, PACK], BF16, name="slotted%d" % i, offset=PLANE_AT[i], align_bytes=64) for i in range(2)]
+        flat2_at = (WOVEN_AT - SHORT_BYTES // 2, FLAT_AT)
+        flat2 = [placed.tile([P, SHORT], BF16, name="flat2_%d" % i, offset=flat2_at[i], align_bytes=64) for i in range(2)]
+        flat3 = placed.tile([P, PAIRED], BF16, name="flat3", offset=FLAT_AT + SHORT_BYTES, align_bytes=64)
+        woven = placed.tile([P, PAIRED * PACK], BF16, name="woven", offset=WOVEN_AT, align_bytes=64)
 
         def picked(j, a, b):
-            return planes[j][:].indirect(picks[:, a // 16 : b // 16])
+            return planes[j][:].indirect(picks[:, a // PER_COLUMN : b // PER_COLUMN])
 
         def pair_gather(j, a, b):
             nc.vector.tensor_copy(pairs[:, j // 2, a:b, j % 2], picked(j, a, b))
+
+        def flat_gather(row, j, a, b):
+            nc.scalar.activation(row, picked(j, PAIRED + a, PAIRED + b), ACT.Copy)
 
         def weave(copy, word, a, b):
             words = pairs[:].rearrange("p u s e -> p u (s e)").bitcast(word)[:, :, a:b]
@@ -91,64 +108,63 @@ def tile_picked_gatv_none_e_kernel(tc, xT, w1_words, w1_scales, score, offs, pos
 
         inv_sums = keep.tile([P, 2], F32, name="inv_sums")
         nc.vector.reciprocal(inv_sums[:], sums[:])
-        pair_gather(0, 0, HALF)
-        nc.scalar.activation(flat01[:, 0, :], picked(0, HALF, S), ACT.Copy)
+        pair_gather(0, 0, PAIRED)
+        flat_gather(flat01[:, 0, :], 0, 0, PAIRED)
         shares = keep.tile([P, 2, D], F32, name="shares")
         nc.vector.tensor_tensor(shares[:], exps[:], inv_sums[:].unsqueeze(2).to_broadcast([P, 2, D]), ALU.mult)
         spread = [psum.tile([P, 2, V], F32, name="spread%d" % b) for b in range(2)]
+        bank_and_slot = ((0, 1), (1, 0), (1, 1), (0, 0))
 
         def share_of(d, a, b):
-            bank, slot = ((0, 1), (1, 0), (1, 1), (0, 0))[d]
+            bank, slot = bank_and_slot[d]
             return spread[bank][:, slot, a:b]
 
         for d in range(D):
             for h in range(2):
                 nc.tensor.transpose(share_of(d, h * P, (h + 1) * P), shares[:, h, d : d + 1].to_broadcast([P, P]), ident[:])
 
-        pair_gather(1, 0, HALF)
+        pair_gather(1, 0, PAIRED)
         for i in range(2):
-            nc.scalar.activation(flat01[:, 1, i * P : (i + 1) * P], picked(1, HALF + i * P, HALF + (i + 1) * P), ACT.Copy)
+            flat_gather(flat01[:, 1, i * P : (i + 1) * P], 1, i * P, (i + 1) * P)
         for i in range(2):
-            nc.vector.tensor_copy(slotted[i][:, :, 0:2], flat01[:, :, i * P : (i + 1) * P].rearrange("p e s -> p s e"))
-        nc.vector.tensor_copy(slotted[1][:, :, 2], picked(2, HALF + P, S))
-        pair_gather(2, 0, HALF)
-        for i, a in enumerate((0, P // 2)):
-            nc.scalar.activation(flat2[i][:], picked(2, HALF + a, HALF + a + P // 2), ACT.Copy)
-        for i, a in enumerate((0, P // 2)):
-            nc.scalar.copy(slotted[0][:, a : a + P // 2, 2], flat2[i][:])
+            nc.vector.tensor_copy(slotted[i][:, :, 0:2], flat01[:, :, i * P : (i + 1) * P].rearrange("p j s -> p s j"))
+
+        nc.vector.tensor_copy(slotted[1][:, :, 2], picked(2, PAIRED + P, S))
+        pair_gather(2, 0, PAIRED)
+        for i in range(2):
+            flat_gather(flat2[i][:], 2, i * SHORT, (i + 1) * SHORT)
+        for i in range(2):
+            nc.scalar.copy(slotted[0][:, i * SHORT : (i + 1) * SHORT, 2], flat2[i][:])
+
         for i in range(2):
             pair_gather(3, i * P, (i + 1) * P)
-        weave(nc.vector.tensor_copy, I32, 0, P // 2)
+        weave(nc.vector.tensor_copy, I32, 0, SHORT)
         for i in range(2):
-            nc.scalar.activation(flat3[:, i * P : (i + 1) * P], picked(3, HALF + i * P, HALF + (i + 1) * P), ACT.Copy)
+            flat_gather(flat3[:, i * P : (i + 1) * P], 3, i * P, (i + 1) * P)
         for i in range(2):
             nc.vector.tensor_copy(slotted[i][:, :, 3], flat3[:, i * P : (i + 1) * P])
-        weave(nc.scalar.copy, U32, P // 2, P)
-        weave(nc.scalar.copy, U32, P, HALF)
-        weights = late.tile([P, FUSED + V], F32, name="weights", offset=0, align_bytes=64)
-        nc.scalar.copy(weights[:], spread[0][:].rearrange("p d v -> p (d v)")[:, V - FUSED : 2 * V])
+        weave(nc.scalar.copy, U32, SHORT, P)
+        weave(nc.scalar.copy, U32, P, PAIRED)
+        fused_shares = placed.tile([P, FUSED + V], F32, name="fused_shares", offset=0, align_bytes=64)
+        nc.scalar.copy(fused_shares[:], spread[0][:].rearrange("p d v -> p (d v)")[:, V - FUSED : 2 * V])
 
         x_scales = keep.tile([P, S], U8, name="x_scales", align_bytes=64)
         y = keep.tile([P, S], F32, name="y")
-        codes = {a: keep.tile([P, P], U32, name="codes%d" % a, align_bytes=64)[:] for a in (0, P, HALF + P)}
-        codes[HALF] = late.tile([P, P], U32, name="codes_first", offset=PLANES_AT + 2 * T * 4, align_bytes=64)[:]
-        order = (HALF, 0, HALF + P, P)
-        grouped = {a: woven[:, a * PACK : (a + P) * PACK] for a in (0, P)}
+        codes = {a: keep.tile([P, P], U32, name="codes%d" % a, align_bytes=64) for a in (0, P, PAIRED + P)}
+        codes[PAIRED] = placed.tile([P, P], U32, name="codes%d" % PAIRED, offset=PLANE_AT[3], align_bytes=64)
+        order = (PAIRED, 0, PAIRED + P, P)
+        interleaved = {a: woven[:, a * PACK : (a + P) * PACK] for a in (0, P)}
         for i in range(2):
-            grouped[HALF + i * P] = slotted[i][:].rearrange("p c j -> p (c j)")
+            interleaved[PAIRED + i * P] = slotted[i][:].rearrange("p s j -> p (s j)")
         for a in order:
-            nc.vector.quantize_mx(
-                out=codes[a].bitcast(FP8X4),
-                scales=x_scales[:, a : a + P],
-                in_=grouped[a],
-            )
+            nc.vector.quantize_mx(out=codes[a][:].bitcast(FP8X4), scales=x_scales[:, a : a + P], in_=interleaved[a])
         for a in order:
             acc = psum.tile([P, P], F32, name="acc%d" % a)
             nc.tensor.matmul_mx(
                 out=acc[:],
                 lhsT=w_codes[:].bitcast(FP8X4),
                 lhsT_scale=w_scales[:],
-                rhs=codes[a].bitcast(FP8X4),
+                rhs=codes[a][:].bitcast(FP8X4),
                 rhs_scale=x_scales[:, a : a + P],
                 start=True,
                 stop=True,
@@ -158,18 +174,19 @@ def tile_picked_gatv_none_e_kernel(tc, xT, w1_words, w1_scales, score, offs, pos
             else:
                 nc.scalar.copy(y[:, a : a + P], acc[:])
 
-        def looked_up(d, a, b):
-            return y[:].indirect(places[d][:, a // 16 : b // 16])
+        def neighbour(d, a, b):
+            return y[:].indirect(places[d][:, a // PER_COLUMN : b // PER_COLUMN])
 
         cut = V - FUSED
-        fetched = [None] + [keep.tile([P, V], F32, name="fetched%d" % d) for d in range(1, D)]
+        fetched = {d: keep.tile([P, V], F32, name="fetched%d" % d) for d in range(1, D)}
         terms = [keep.tile([P, V], F32, name="terms%d" % d) for d in range(D)]
-        totals = [keep.tile([P, V], F32, name="totals%d" % d) for d in range(2)]
+        partial = keep.tile([P, V], F32, name="partial")
+        result = keep.tile([P, V], F32, name="result")
         for d in range(1, D):
             for a, b in ((0, P), (P, V if d < D - 1 else cut)):
-                nc.scalar.activation(fetched[d][:, a:b], looked_up(d, a, b), ACT.Copy)
-        nc.vector.tensor_tensor(terms[0][:], looked_up(0, 0, V), weights[:, FUSED:], ALU.mult)
-        nc.vector.tensor_tensor(terms[3][:, cut:V], looked_up(3, cut, V), weights[:, 0:FUSED], ALU.mult)
+                nc.scalar.activation(fetched[d][:, a:b], neighbour(d, a, b), ACT.Copy)
+        nc.vector.tensor_tensor(terms[0][:], neighbour(0, 0, V), fused_shares[:, FUSED:], ALU.mult)
+        nc.vector.tensor_tensor(terms[3][:, cut:V], neighbour(3, cut, V), fused_shares[:, 0:FUSED], ALU.mult)
 
         def weigh(d, a, b):
             nc.vector.tensor_tensor(terms[d][:, a:b], fetched[d][:, a:b], share_of(d, a, b), ALU.mult)
@@ -180,17 +197,17 @@ def tile_picked_gatv_none_e_kernel(tc, xT, w1_words, w1_scales, score, offs, pos
         weigh(1, 0, P)
         weigh(1, P, V)
         add(terms[0], terms[0], 3, cut, V)
-        add(totals[0], terms[0], 1, 0, P)
+        add(partial, terms[0], 1, 0, P)
         weigh(2, 0, P)
-        add(totals[0], terms[0], 1, P, V)
+        add(partial, terms[0], 1, P, V)
         weigh(2, P, V)
-        add(totals[1], totals[0], 2, 0, P)
+        add(result, partial, 2, 0, P)
         weigh(3, 0, P)
-        add(totals[1], totals[0], 2, P, cut)
+        add(result, partial, 2, P, cut)
         weigh(3, P, cut)
-        add(totals[1], totals[0], 2, cut, V)
-        add(totals[1], totals[1], 3, 0, P)
-        add(totals[1], totals[1], 3, P, cut)
-        nc.scalar.dma_start(out=out[:, cut:V], in_=totals[1][:, cut:V])
-        nc.scalar.dma_start(out=out[:, 0:P], in_=totals[1][:, 0:P])
-        nc.sync.dma_start(out=out[:, P:cut], in_=totals[1][:, P:cut])
+        add(result, partial, 2, cut, V)
+        add(result, result, 3, 0, P)
+        add(result, result, 3, P, cut)
+        nc.scalar.dma_start(out=out[:, cut:V], in_=result[:, cut:V])
+        nc.scalar.dma_start(out=out[:, 0:P], in_=result[:, 0:P])
+        nc.sync.dma_start(out=out[:, P:cut], in_=result[:, P:cut])

@@ -23,12 +23,12 @@ FUSED = 64
 SCORE_ROWS = 2 * D
 FIRST_SCORE_ROW = P - SCORE_ROWS
 
-PIECE_BYTES = P * PACK * 2
-PLANE_BYTES = T * 4
-PLANE_AT = [2 * PIECE_BYTES + place * PLANE_BYTES for place in (0, 3, 1, 2)]
-SHORT_BYTES = SHORT * 2
-FLAT_AT = PLANE_AT[1] + 2 * PIECE_BYTES
-WOVEN_AT = FLAT_AT + SHORT_BYTES + PAIRED * 2
+PAIRS_AT = 0
+PAIR_VALUES = PAIRED * PACK
+ROW0_FROM = PAIR_VALUES - PAIRED - P
+ROW_STEP = PAIR_VALUES + PAIRED - ROW0_FROM
+STAGED_VALUES = ROW0_FROM + 2 * ROW_STEP
+LAST_PLANE_AT = PAIRS_AT + STAGED_VALUES * 2
 
 FLOPS = 2 * K * S * N
 BYTES = 4 * K * T + K * N + K * N // 32 + 4 * D * V + 2 * (S + D * V) + 4 * N * V
@@ -46,23 +46,21 @@ def tile_picked_gatv_none_e_kernel(tc, xT, w1_words, w1_scales, score, offs, pos
         half_rows = score.rearrange("d p (h c) -> (d p h) c", c=P)
         nc.scalar.dma_start(out=score_rows[FIRST_SCORE_ROW:P, :], in_=half_rows[0 : D * P * 2 : P + 1, :])
         nc.vector.memset(score_rows[0:FIRST_SCORE_ROW, :], 0.0)
-        x_planes = xT.rearrange("(p j) t -> j p t", j=PACK)
-        planes = [placed.tile([P, T], F32, name="plane%d" % j, offset=PLANE_AT[j], align_bytes=64) for j in range(PACK)]
-        picks = lists.tile([P, S // PER_COLUMN], U16, name="picks")
-        nc.sync.dma_start(out=planes[0][:], in_=x_planes[0])
-        nc.sync.dma_start(picks[:], offs)
-        for j in range(1, PACK):
-            nc.sync.dma_start(out=planes[j][:], in_=x_planes[j])
-        w_codes = keep.tile([P, N], U32, name="w_codes", align_bytes=64)
-        nc.sync.dma_start(out=w_codes[:].bitcast(I32), in_=w1_words[0].rearrange("p n t -> p (n t)").bitcast(I32))
         w_scales = keep.tile([P, N], U8, name="w_scales", align_bytes=64)
         nc.vector.memset(w_scales[:].bitcast(I32), 0)
-
-        def load_scale_rows(queue, q):
-            queue.dma_start(out=w_scales[32 * q : 32 * q + 4, :].bitcast(I32), in_=w1_scales[0, 4 * q : 4 * q + 4, :].bitcast(I32))
-
-        for q in (0, 1):
-            load_scale_rows(nc.sync, q)
+        x_rows = xT.rearrange("(p j) t -> p (j t)", j=PACK)
+        early = [keep.tile([P, T], F32, name="early%d" % j, align_bytes=64) for j in range(PACK - 1)]
+        last = placed.tile([P, T], F32, name="last", offset=LAST_PLANE_AT, align_bytes=64)
+        planes = [plane[:] for plane in early + [last]]
+        picks = lists.tile([P, S // PER_COLUMN], U16, name="picks")
+        nc.sync.dma_start(out=planes[0], in_=x_rows[:, 0:T])
+        nc.sync.dma_start(picks[:], offs)
+        for j in range(1, PACK):
+            nc.sync.dma_start(out=planes[j], in_=x_rows[:, j * T : (j + 1) * T])
+        w_codes = keep.tile([P, N], U32, name="w_codes", align_bytes=64)
+        nc.sync.dma_start(out=w_codes[:].bitcast(I32), in_=w1_words[0].rearrange("p n t -> p (n t)").bitcast(I32))
+        for q in range(4):
+            nc.sync.dma_start(out=w_scales[32 * q : 32 * q + 4, :].bitcast(I32), in_=w1_scales[0, 4 * q : 4 * q + 4, :].bitcast(I32))
         places = []
         for d, pos in enumerate((pos1, pos2, pos3, pos4)):
             place = lists.tile([P, V // PER_COLUMN], U16, name="place%d" % d)
@@ -71,45 +69,19 @@ def tile_picked_gatv_none_e_kernel(tc, xT, w1_words, w1_scales, score, offs, pos
 
         ident = keep.tile([P, P], F32, name="ident")
         make_identity(nc, ident[:])
-        for q in (2, 3):
-            load_scale_rows(nc.gpsimd, q)
 
         score_bank = psum.tile([P, P], F32, name="score_bank")
         nc.tensor.transpose(score_bank[:], score_rows[:], ident[:])
         scores = score_bank[:, FIRST_SCORE_ROW:P].rearrange("p (d h) -> p h d", h=2)
-        minus_largest = placed.tile([P, 2], F32, name="minus_largest", offset=0, align_bytes=64)
+        maxima = placed.tile([P, 2], F32, name="maxima", offset=PAIRS_AT, align_bytes=64)
+        minus_largest = maxima[:]
         sums = keep.tile([P, 2], F32, name="sums")
-        nc.vector.tensor_reduce(minus_largest[:], scores, mybir.AxisListType.X, ALU.max, negate=True)
+        nc.vector.tensor_reduce(minus_largest, scores, mybir.AxisListType.X, ALU.max, negate=True)
         exps = keep.tile([P, 2, D], F32, name="exps")
         for h in range(2):
             nc.scalar.activation(exps[:, h, :], scores[:, h, :], ACT.Exp, bias=minus_largest[:, h : h + 1], accum_out=sums[:, h : h + 1])
-
-        pairs = placed.tile([P, 2, PAIRED, 2], BF16, name="pairs", offset=0, align_bytes=64)
-        flat01 = pairs[:, 1, :, :].rearrange("p s e -> p (s e)").rearrange("p (j s) -> p j s", j=2)
-        slotted = [placed.tile([P, P, PACK], BF16, name="slotted%d" % i, offset=PLANE_AT[i], align_bytes=64) for i in range(2)]
-        flat2_at = (WOVEN_AT - SHORT_BYTES // 2, FLAT_AT)
-        flat2 = [placed.tile([P, SHORT], BF16, name="flat2_%d" % i, offset=flat2_at[i], align_bytes=64) for i in range(2)]
-        flat3 = placed.tile([P, PAIRED], BF16, name="flat3", offset=FLAT_AT + SHORT_BYTES, align_bytes=64)
-        woven = placed.tile([P, PAIRED * PACK], BF16, name="woven", offset=WOVEN_AT, align_bytes=64)
-
-        def picked(j, a, b):
-            return planes[j][:].indirect(picks[:, a // PER_COLUMN : b // PER_COLUMN])
-
-        def pair_gather(j, a, b):
-            nc.vector.tensor_copy(pairs[:, j // 2, a:b, j % 2], picked(j, a, b))
-
-        def flat_gather(row, j, a, b):
-            nc.scalar.activation(row, picked(j, PAIRED + a, PAIRED + b), ACT.Copy)
-
-        def weave(copy, word, a, b):
-            words = pairs[:].rearrange("p u s e -> p u (s e)").bitcast(word)[:, :, a:b]
-            dst = woven[:, a * PACK : b * PACK].bitcast(word)
-            copy(dst.rearrange("p (s u) -> p s u", u=2), words.rearrange("p u s -> p s u"))
-
         inv_sums = keep.tile([P, 2], F32, name="inv_sums")
         nc.vector.reciprocal(inv_sums[:], sums[:])
-        pair_gather(0, 0, PAIRED)
-        flat_gather(flat01[:, 0, :], 0, 0, PAIRED)
         shares = keep.tile([P, 2, D], F32, name="shares")
         nc.vector.tensor_tensor(shares[:], exps[:], inv_sums[:].unsqueeze(2).to_broadcast([P, 2, D]), ALU.mult)
         spread = [psum.tile([P, 2, V], F32, name="spread%d" % b) for b in range(2)]
@@ -123,39 +95,58 @@ def tile_picked_gatv_none_e_kernel(tc, xT, w1_words, w1_scales, score, offs, pos
             for h in range(2):
                 nc.tensor.transpose(share_of(d, h * P, (h + 1) * P), shares[:, h, d : d + 1].to_broadcast([P, P]), ident[:])
 
-        pair_gather(1, 0, PAIRED)
-        for i in range(2):
-            flat_gather(flat01[:, 1, i * P : (i + 1) * P], 1, i * P, (i + 1) * P)
-        for i in range(2):
-            nc.vector.tensor_copy(slotted[i][:, :, 0:2], flat01[:, :, i * P : (i + 1) * P].rearrange("p j s -> p s j"))
+        staged = placed.tile([P, STAGED_VALUES], BF16, name="staged", offset=PAIRS_AT, align_bytes=64)
+        pairs = staged[:, 0:PAIR_VALUES].rearrange("p (u s e) -> p u s e", u=2, e=2)
+        flat01 = staged[:, ROW0_FROM:].rearrange("p (j s) -> p j s", j=2)[:, :, 0:PAIRED]
+        flat23 = staged[:, PAIR_VALUES : PAIR_VALUES + 2 * PAIRED].rearrange("p (j s) -> p j s", j=2)
+        slotted = keep.tile([P, PAIRED, PACK], BF16, name="slotted", align_bytes=64)
+        woven = keep.tile([P, PAIRED * PACK], BF16, name="woven", align_bytes=64)
 
-        nc.vector.tensor_copy(slotted[1][:, :, 2], picked(2, PAIRED + P, S))
+        def picked(j, a, b):
+            return planes[j].indirect(picks[:, a // PER_COLUMN : b // PER_COLUMN])
+
+        def pair_gather(j, a, b):
+            nc.vector.tensor_copy(pairs[:, j // 2, a:b, j % 2], picked(j, a, b))
+
+        def flat_gather(j, a, b):
+            rows = (flat01, flat23)[j // 2]
+            nc.scalar.activation(rows[:, j % 2, a:b], picked(j, PAIRED + a, PAIRED + b), ACT.Copy)
+
+        def fill_slots(u, a, b):
+            rows = (flat01, flat23)[u]
+            nc.vector.tensor_copy(slotted[:, a:b, 2 * u : 2 * u + 2], rows[:, :, a:b].rearrange("p j s -> p s j"))
+
+        def weave(copy, word, a, b):
+            words = pairs.rearrange("p u s e -> p u (s e)").bitcast(word)[:, :, a:b]
+            dst = woven[:, a * PACK : b * PACK].bitcast(word)
+            copy(dst.rearrange("p (s u) -> p s u", u=2), words.rearrange("p u s -> p s u"))
+
+        for j in range(2):
+            pair_gather(j, 0, PAIRED)
+            flat_gather(j, 0, PAIRED)
+        fill_slots(0, 0, PAIRED)
         pair_gather(2, 0, PAIRED)
-        for i in range(2):
-            flat_gather(flat2[i][:], 2, i * SHORT, (i + 1) * SHORT)
-        for i in range(2):
-            nc.scalar.copy(slotted[0][:, i * SHORT : (i + 1) * SHORT, 2], flat2[i][:])
+        flat_gather(2, 0, PAIRED)
 
         for i in range(2):
             pair_gather(3, i * P, (i + 1) * P)
-        weave(nc.vector.tensor_copy, I32, 0, SHORT)
         for i in range(2):
-            flat_gather(flat3[:, i * P : (i + 1) * P], 3, i * P, (i + 1) * P)
+            flat_gather(3, i * P, (i + 1) * P)
         for i in range(2):
-            nc.vector.tensor_copy(slotted[i][:, :, 3], flat3[:, i * P : (i + 1) * P])
-        weave(nc.scalar.copy, U32, SHORT, P)
-        weave(nc.scalar.copy, U32, P, PAIRED)
-        fused_shares = placed.tile([P, FUSED + V], F32, name="fused_shares", offset=0, align_bytes=64)
+            fill_slots(1, i * P, (i + 1) * P)
+        for i in range(2):
+            weave(nc.scalar.copy, U32, i * P, (i + 1) * P)
+        fused_shares = placed.tile([P, FUSED + V], F32, name="fused_shares", offset=PAIRS_AT, align_bytes=64)
         nc.scalar.copy(fused_shares[:], spread[0][:].rearrange("p d v -> p (d v)")[:, V - FUSED : 2 * V])
 
         x_scales = keep.tile([P, S], U8, name="x_scales", align_bytes=64)
         y = keep.tile([P, S], F32, name="y")
         codes = {a: keep.tile([P, P], U32, name="codes%d" % a, align_bytes=64) for a in (0, P, PAIRED + P)}
-        codes[PAIRED] = placed.tile([P, P], U32, name="codes%d" % PAIRED, offset=PLANE_AT[3], align_bytes=64)
+        codes[PAIRED] = placed.tile([P, P], U32, name="codes%d" % PAIRED, offset=LAST_PLANE_AT, align_bytes=64)
         order = (PAIRED, 0, PAIRED + P, P)
         interleaved = {a: woven[:, a * PACK : (a + P) * PACK] for a in (0, P)}
         for i in range(2):
-            interleaved[PAIRED + i * P] = slotted[i][:].rearrange("p s j -> p (s j)")
+            interleaved[PAIRED + i * P] = slotted[:, i * P : (i + 1) * P, :].rearrange("p s j -> p (s j)")
         for a in order:
             nc.vector.quantize_mx(out=codes[a][:].bitcast(FP8X4), scales=x_scales[:, a : a + P], in_=interleaved[a])
         for a in order:
@@ -208,6 +199,4 @@ def tile_picked_gatv_none_e_kernel(tc, xT, w1_words, w1_scales, score, offs, pos
         add(result, partial, 2, cut, V)
         add(result, result, 3, 0, P)
         add(result, result, 3, P, cut)
-        nc.scalar.dma_start(out=out[:, cut:V], in_=result[:, cut:V])
-        nc.scalar.dma_start(out=out[:, 0:P], in_=result[:, 0:P])
-        nc.sync.dma_start(out=out[:, P:cut], in_=result[:, P:cut])
+        nc.sync.dma_start(out=out[:, :], in_=result[:])

@@ -19,7 +19,7 @@ PACK = 4
 PAIRED = S // 2
 PER_COLUMN = 16
 SHORT = P // 2
-FUSED = 64
+FUSED = 128
 SCORE_ROWS = 2 * D
 FIRST_SCORE_ROW = P - SCORE_ROWS
 
@@ -173,9 +173,8 @@ def tile_picked_gatv_none_e_kernel(tc, xT, w1_words, w1_scales, score, offs, pos
         terms = [keep.tile([P, V], F32, name="terms%d" % d) for d in range(D)]
         partial = keep.tile([P, V], F32, name="partial")
         result = keep.tile([P, V], F32, name="result")
-        for d in range(1, D):
-            for a, b in ((0, P), (P, V if d < D - 1 else cut)):
-                nc.scalar.activation(fetched[d][:, a:b], neighbour(d, a, b), ACT.Copy)
+        for d, a, b in ((1, 0, V), (3, 0, cut), (2, 0, P), (2, P, V)):
+            nc.scalar.activation(fetched[d][:, a:b], neighbour(d, a, b), ACT.Copy)
         nc.vector.tensor_tensor(terms[0][:], neighbour(0, 0, V), fused_shares[:, FUSED:], ALU.mult)
         nc.vector.tensor_tensor(terms[3][:, cut:V], neighbour(3, cut, V), fused_shares[:, 0:FUSED], ALU.mult)
 
@@ -185,18 +184,14 @@ def tile_picked_gatv_none_e_kernel(tc, xT, w1_words, w1_scales, score, offs, pos
         def add(dst, src, d, a, b):
             nc.vector.tensor_tensor(dst[:, a:b], src[:, a:b], terms[d][:, a:b], ALU.add)
 
-        weigh(1, 0, P)
-        weigh(1, P, V)
+        weigh(1, 0, V)
+        weigh(3, 0, cut)
         add(terms[0], terms[0], 3, cut, V)
         add(partial, terms[0], 1, 0, P)
         weigh(2, 0, P)
         add(partial, terms[0], 1, P, V)
         weigh(2, P, V)
+        add(partial, partial, 3, 0, P)
+        add(result, partial, 2, P, V)
         add(result, partial, 2, 0, P)
-        weigh(3, 0, P)
-        add(result, partial, 2, P, cut)
-        weigh(3, P, cut)
-        add(result, partial, 2, cut, V)
-        add(result, result, 3, 0, P)
-        add(result, result, 3, P, cut)
         nc.sync.dma_start(out=out[:, :], in_=result[:])

@@ -45,9 +45,9 @@ def tile_picked_gatv_none_e_kernel(tc, xT, w1_words, w1_scales, score, offs, pos
         score_rows = keep.tile([P, P], F32, name="score_rows")
         half_rows = score.rearrange("d p (h c) -> (d p h) c", c=P)
         nc.scalar.dma_start(out=score_rows[FIRST_SCORE_ROW:P, :], in_=half_rows[0 : D * P * 2 : P + 1, :])
-        nc.vector.memset(score_rows[0:FIRST_SCORE_ROW, :], 0.0)
         w_scales = keep.tile([P, N], U8, name="w_scales", align_bytes=64)
         nc.vector.memset(w_scales[:].bitcast(I32), 0)
+        nc.vector.memset(score_rows[0:FIRST_SCORE_ROW, :], 0.0)
         x_rows = xT.rearrange("(p j) t -> p (j t)", j=PACK)
         early = [keep.tile([P, T], F32, name="early%d" % j, align_bytes=64) for j in range(PACK - 1)]
         last = placed.tile([P, T], F32, name="last", offset=LAST_PLANE_AT, align_bytes=64)
@@ -58,14 +58,17 @@ def tile_picked_gatv_none_e_kernel(tc, xT, w1_words, w1_scales, score, offs, pos
         for j in range(1, PACK):
             nc.sync.dma_start(out=planes[j], in_=x_rows[:, j * T : (j + 1) * T])
         w_codes = keep.tile([P, N], U32, name="w_codes", align_bytes=64)
-        nc.sync.dma_start(out=w_codes[:].bitcast(I32), in_=w1_words[0].rearrange("p n t -> p (n t)").bitcast(I32))
-        for q in range(4):
+
+        def load_scale_rows(q):
             nc.sync.dma_start(out=w_scales[32 * q : 32 * q + 4, :].bitcast(I32), in_=w1_scales[0, 4 * q : 4 * q + 4, :].bitcast(I32))
-        places = []
-        for d, pos in enumerate((pos1, pos2, pos3, pos4)):
-            place = lists.tile([P, V // PER_COLUMN], U16, name="place%d" % d)
-            nc.sync.dma_start(place[:], pos)
-            places.append(place)
+
+        load_scale_rows(0)
+        nc.sync.dma_start(out=w_codes[:].bitcast(I32), in_=w1_words[0].rearrange("p n t -> p (n t)").bitcast(I32))
+        for q in range(1, 4):
+            load_scale_rows(q)
+        places = [lists.tile([P, V // PER_COLUMN], U16, name="place%d" % d) for d in range(D)]
+        for d in (0, 1, 3, 2):
+            nc.sync.dma_start(places[d][:], (pos1, pos2, pos3, pos4)[d])
 
         ident = keep.tile([P, P], F32, name="ident")
         make_identity(nc, ident[:])

@@ -23,12 +23,12 @@ FUSED = 128
 SCORE_ROWS = 2 * D
 FIRST_SCORE_ROW = P - SCORE_ROWS
 
-PAIRS_AT = 0
-PAIR_VALUES = PAIRED * PACK
-ROW0_FROM = PAIR_VALUES - PAIRED - P
-ROW_STEP = PAIR_VALUES + PAIRED - ROW0_FROM
-STAGED_VALUES = ROW0_FROM + 2 * ROW_STEP
-LAST_PLANE_AT = PAIRS_AT + STAGED_VALUES * 2
+STAGED_AT = 0
+PAIR_WORDS = 2 * PAIRED
+FLAT_WORDS = PAIRED // 2 + 2 * PAIRED
+STAGED_WORDS = PAIR_WORDS + FLAT_WORDS
+LAST_PLANE_AT = STAGED_AT + STAGED_WORDS * 4
+BY_VECTOR = PAIRED - SHORT
 
 FLOPS = 2 * K * S * N
 BYTES = 4 * K * T + K * N + K * N // 32 + 4 * D * V + 2 * (S + D * V) + 4 * N * V
@@ -49,13 +49,14 @@ def tile_picked_gatv_none_e_kernel(tc, xT, w1_words, w1_scales, score, offs, pos
         nc.vector.memset(w_scales[:].bitcast(I32), 0)
         nc.vector.memset(score_rows[0:FIRST_SCORE_ROW, :], 0.0)
         x_rows = xT.rearrange("(p j) t -> p (j t)", j=PACK)
-        early = [keep.tile([P, T], F32, name="early%d" % j, align_bytes=64) for j in range(PACK - 1)]
+        first_two = keep.tile([P, 2 * T], F32, name="first_two", align_bytes=64)
+        third = keep.tile([P, T], F32, name="third", align_bytes=64)
         last = placed.tile([P, T], F32, name="last", offset=LAST_PLANE_AT, align_bytes=64)
-        planes = [plane[:] for plane in early + [last]]
+        planes = [first_two[:, 0:T], first_two[:, T : 2 * T], third[:], last[:]]
         picks = lists.tile([P, S // PER_COLUMN], U16, name="picks")
-        nc.sync.dma_start(out=planes[0], in_=x_rows[:, 0:T])
+        nc.sync.dma_start(out=first_two[:], in_=x_rows[:, 0 : 2 * T])
         nc.sync.dma_start(picks[:], offs)
-        for j in range(1, PACK):
+        for j in range(2, PACK):
             nc.sync.dma_start(out=planes[j], in_=x_rows[:, j * T : (j + 1) * T])
         w_codes = keep.tile([P, N], U32, name="w_codes", align_bytes=64)
 
@@ -76,17 +77,18 @@ def tile_picked_gatv_none_e_kernel(tc, xT, w1_words, w1_scales, score, offs, pos
         score_bank = psum.tile([P, P], F32, name="score_bank")
         nc.tensor.transpose(score_bank[:], score_rows[:], ident[:])
         scores = score_bank[:, FIRST_SCORE_ROW:P].rearrange("p (d h) -> p h d", h=2)
-        maxima = placed.tile([P, 2], F32, name="maxima", offset=PAIRS_AT, align_bytes=64)
+        maxima = placed.tile([P, 2], F32, name="maxima", offset=STAGED_AT + PAIR_WORDS * 4, align_bytes=64)
         minus_largest = maxima[:]
         sums = keep.tile([P, 2], F32, name="sums")
         nc.vector.tensor_reduce(minus_largest, scores, mybir.AxisListType.X, ALU.max, negate=True)
-        exps = keep.tile([P, 2, D], F32, name="exps")
+        exps = placed.tile([P, 2, D], F32, name="exps", offset=STAGED_AT, align_bytes=64)
         for h in range(2):
             nc.scalar.activation(exps[:, h, :], scores[:, h, :], ACT.Exp, bias=minus_largest[:, h : h + 1], accum_out=sums[:, h : h + 1])
-        inv_sums = keep.tile([P, 2], F32, name="inv_sums")
-        nc.vector.reciprocal(inv_sums[:], sums[:])
+        flats = placed.tile([P, FLAT_WORDS], F32, name="flats", offset=STAGED_AT + PAIR_WORDS * 4, align_bytes=64)
+        inv_sums = flats[:, 0:2]
+        nc.vector.reciprocal(inv_sums, sums[:])
         shares = keep.tile([P, 2, D], F32, name="shares")
-        nc.vector.tensor_tensor(shares[:], exps[:], inv_sums[:].unsqueeze(2).to_broadcast([P, 2, D]), ALU.mult)
+        nc.vector.tensor_tensor(shares[:], exps[:], inv_sums.unsqueeze(2).to_broadcast([P, 2, D]), ALU.mult)
         spread = [psum.tile([P, 2, V], F32, name="spread%d" % b) for b in range(2)]
         bank_and_slot = ((0, 1), (1, 0), (1, 1), (0, 0))
 
@@ -98,10 +100,10 @@ def tile_picked_gatv_none_e_kernel(tc, xT, w1_words, w1_scales, score, offs, pos
             for h in range(2):
                 nc.tensor.transpose(share_of(d, h * P, (h + 1) * P), shares[:, h, d : d + 1].to_broadcast([P, P]), ident[:])
 
-        staged = placed.tile([P, STAGED_VALUES], BF16, name="staged", offset=PAIRS_AT, align_bytes=64)
-        pairs = staged[:, 0:PAIR_VALUES].rearrange("p (u s e) -> p u s e", u=2, e=2)
-        flat01 = staged[:, ROW0_FROM:].rearrange("p (j s) -> p j s", j=2)[:, :, 0:PAIRED]
-        flat23 = staged[:, PAIR_VALUES : PAIR_VALUES + 2 * PAIRED].rearrange("p (j s) -> p j s", j=2)
+        pair_tile = placed.tile([P, 2, PAIRED, 2], BF16, name="pair_tile", offset=STAGED_AT, align_bytes=64)
+        pairs = pair_tile[:]
+        flat01 = flats[:, PAIRED // 2 :].rearrange("p (j s) -> p j s", j=2)
+        flat23 = flats[:, 0:PAIRED].bitcast(BF16).rearrange("p (j s) -> p j s", j=2)
         slotted = keep.tile([P, PAIRED, PACK], BF16, name="slotted", align_bytes=64)
         woven = keep.tile([P, PAIRED * PACK], BF16, name="woven", align_bytes=64)
 
@@ -115,31 +117,34 @@ def tile_picked_gatv_none_e_kernel(tc, xT, w1_words, w1_scales, score, offs, pos
             rows = (flat01, flat23)[j // 2]
             nc.scalar.activation(rows[:, j % 2, a:b], picked(j, PAIRED + a, PAIRED + b), ACT.Copy)
 
-        def fill_slots(u, a, b):
+        def fill_slots(copy, u, a, b):
             rows = (flat01, flat23)[u]
-            nc.vector.tensor_copy(slotted[:, a:b, 2 * u : 2 * u + 2], rows[:, :, a:b].rearrange("p j s -> p s j"))
+            copy(slotted[:, a:b, 2 * u : 2 * u + 2], rows[:, :, a:b].rearrange("p j s -> p s j"))
 
         def weave(copy, word, a, b):
             words = pairs.rearrange("p u s e -> p u (s e)").bitcast(word)[:, :, a:b]
             dst = woven[:, a * PACK : b * PACK].bitcast(word)
             copy(dst.rearrange("p (s u) -> p s u", u=2), words.rearrange("p u s -> p s u"))
 
-        for j in range(2):
+        for j in range(PACK - 1):
             pair_gather(j, 0, PAIRED)
-            flat_gather(j, 0, PAIRED)
-        fill_slots(0, 0, PAIRED)
-        pair_gather(2, 0, PAIRED)
-        flat_gather(2, 0, PAIRED)
+        nc.vector.tensor_copy(flat23[:, 0, 0:BY_VECTOR], picked(2, PAIRED, PAIRED + BY_VECTOR))
+        for i in range(2):
+            for j in range(2):
+                flat_gather(j, i * P, (i + 1) * P)
+        for i in range(2):
+            fill_slots(nc.scalar.copy, 0, i * P, (i + 1) * P)
+        flat_gather(2, BY_VECTOR, PAIRED)
 
         for i in range(2):
             pair_gather(3, i * P, (i + 1) * P)
         for i in range(2):
             flat_gather(3, i * P, (i + 1) * P)
         for i in range(2):
-            fill_slots(1, i * P, (i + 1) * P)
+            fill_slots(nc.vector.tensor_copy, 1, i * P, (i + 1) * P)
         for i in range(2):
             weave(nc.scalar.copy, U32, i * P, (i + 1) * P)
-        fused_shares = placed.tile([P, FUSED + V], F32, name="fused_shares", offset=PAIRS_AT, align_bytes=64)
+        fused_shares = placed.tile([P, FUSED + V], F32, name="fused_shares", offset=STAGED_AT, align_bytes=64)
         nc.scalar.copy(fused_shares[:], spread[0][:].rearrange("p d v -> p (d v)")[:, V - FUSED : 2 * V])
 
         x_scales = keep.tile([P, S], U8, name="x_scales", align_bytes=64)

from contextlib import ExitStack

import concourse.mybir as mybir
from concourse.masks import make_identity

F32 = mybir.dt.float32
BF16 = mybir.dt.bfloat16
I32 = mybir.dt.int32
U32 = mybir.dt.uint32
U16 = mybir.dt.uint16
U8 = mybir.dt.uint8
FP8X4 = mybir.dt.float8_e4m3fn_x4
ALU = mybir.AluOpType
ACT = mybir.ActivationFunctionType

P = 128
K, T, S, D, V, N = 512, 1024, 512, 4, 256, 128
PACK = 4
PAIRED = S // 2
PER_COLUMN = 16
SHORT = P // 2
FUSED = 128
SCORE_ROWS = 2 * D
FIRST_SCORE_ROW = P - SCORE_ROWS

STAGED_AT = 0
PAIR_WORDS = 2 * PAIRED
FLAT_WORDS = PAIRED // 2 + 2 * PAIRED
STAGED_WORDS = PAIR_WORDS + FLAT_WORDS
LAST_PLANE_AT = STAGED_AT + STAGED_WORDS * 4
BY_VECTOR = PAIRED - SHORT

FLOPS = 2 * K * S * N
BYTES = 4 * K * T + K * N + K * N // 32 + 4 * D * V + 2 * (S + D * V) + 4 * N * V


def tile_picked_gatv_none_e_kernel(tc, xT, w1_words, w1_scales, score, offs, pos1, pos2, pos3, pos4, out):
    nc = tc.nc
    with ExitStack() as ctx:
        lists = ctx.enter_context(tc.tile_pool(name="lists", bufs=1))
        keep = ctx.enter_context(tc.tile_pool(name="keep", bufs=1))
        placed = ctx.enter_context(tc.tile_pool(name="placed", bufs=1))
        psum = ctx.enter_context(tc.psum_pool(name="psum", bufs=1))

        score_rows = keep.tile([P, P], F32, name="score_rows")
        half_rows = score.rearrange("d p (h c) -> (d p h) c", c=P)
        nc.scalar.dma_start(out=score_rows[FIRST_SCORE_ROW:P, :], in_=half_rows[0 : D * P * 2 : P + 1, :])
        w_scales = keep.tile([P, N], U8, name="w_scales", align_bytes=64)
        nc.vector.memset(w_scales[:].bitcast(I32), 0)
        nc.vector.memset(score_rows[0:FIRST_SCORE_ROW, :], 0.0)
        x_rows = xT.rearrange("(p j) t -> p (j t)", j=PACK)
        first_two = keep.tile([P, 2 * T], F32, name="first_two", align_bytes=64)
        third = keep.tile([P, T], F32, name="third", align_bytes=64)
        last = placed.tile([P, T], F32, name="last", offset=LAST_PLANE_AT, align_bytes=64)
        planes = [first_two[:, 0:T], first_two[:, T : 2 * T], third[:], last[:]]
        picks = lists.tile([P, S // PER_COLUMN], U16, name="picks")
        nc.sync.dma_start(out=first_two[:], in_=x_rows[:, 0 : 2 * T])
        nc.sync.dma_start(picks[:], offs)
        for j in range(2, PACK):
            nc.sync.dma_start(out=planes[j], in_=x_rows[:, j * T : (j + 1) * T])
        w_codes = keep.tile([P, N], U32, name="w_codes", align_bytes=64)

        def load_scale_rows(q):
            nc.sync.dma_start(out=w_scales[32 * q : 32 * q + 4, :].bitcast(I32), in_=w1_scales[0, 4 * q : 4 * q + 4, :].bitcast(I32))

        load_scale_rows(0)
        nc.sync.dma_start(out=w_codes[:].bitcast(I32), in_=w1_words[0].rearrange("p n t -> p (n t)").bitcast(I32))
        for q in range(1, 4):
            load_scale_rows(q)
        places = [lists.tile([P, V // PER_COLUMN], U16, name="place%d" % d) for d in range(D)]
        for d in (0, 1, 3, 2):
            nc.sync.dma_start(places[d][:], (pos1, pos2, pos3, pos4)[d])

        ident = keep.tile([P, P], F32, name="ident")
        make_identity(nc, ident[:])

        score_bank = psum.tile([P, P], F32, name="score_bank")
        nc.tensor.transpose(score_bank[:], score_rows[:], ident[:])
        scores = score_bank[:, FIRST_SCORE_ROW:P].rearrange("p (d h) -> p h d", h=2)
        maxima = placed.tile([P, 2], F32, name="maxima", offset=STAGED_AT + PAIR_WORDS * 4, align_bytes=64)
        minus_largest = maxima[:]
        sums = keep.tile([P, 2], F32, name="sums")
        nc.vector.tensor_reduce(minus_largest, scores, mybir.AxisListType.X, ALU.max, negate=True)
        exps = placed.tile([P, 2, D], F32, name="exps", offset=STAGED_AT, align_bytes=64)
        for h in range(2):
            nc.scalar.activation(exps[:, h, :], scores[:, h, :], ACT.Exp, bias=minus_largest[:, h : h + 1], accum_out=sums[:, h : h + 1])
        flats = placed.tile([P, FLAT_WORDS], F32, name="flats", offset=STAGED_AT + PAIR_WORDS * 4, align_bytes=64)
        inv_sums = flats[:, 0:2]
        nc.vector.reciprocal(inv_sums, sums[:])
        shares = keep.tile([P, 2, D], F32, name="shares")
        nc.vector.tensor_tensor(shares[:], exps[:], inv_sums.unsqueeze(2).to_broadcast([P, 2, D]), ALU.mult)
        spread = [psum.tile([P, 2, V], F32, name="spread%d" % b) for b in range(2)]
        bank_and_slot = ((0, 1), (1, 0), (1, 1), (0, 0))

        def share_of(d, a, b):
            bank, slot = bank_and_slot[d]
            return spread[bank][:, slot, a:b]

        for d in range(D):
            for h in range(2):
                nc.tensor.transpose(share_of(d, h * P, (h + 1) * P), shares[:, h, d : d + 1].to_broadcast([P, P]), ident[:])

        pair_tile = placed.tile([P, 2, PAIRED, 2], BF16, name="pair_tile", offset=STAGED_AT, align_bytes=64)
        pairs = pair_tile[:]
        flat01 = flats[:, PAIRED // 2 :].rearrange("p (j s) -> p j s", j=2)
        flat23 = flats[:, 0:PAIRED].bitcast(BF16).rearrange("p (j s) -> p j s", j=2)
        slotted = keep.tile([P, PAIRED, PACK], BF16, name="slotted", align_bytes=64)
        woven = keep.tile([P, PAIRED * PACK], BF16, name="woven", align_bytes=64)

        def picked(j, a, b):
            return planes[j].indirect(picks[:, a // PER_COLUMN : b // PER_COLUMN])

        def pair_gather(j, a, b):
            nc.vector.tensor_copy(pairs[:, j // 2, a:b, j % 2], picked(j, a, b))

        def flat_gather(j, a, b):
            rows = (flat01, flat23)[j // 2]
            nc.scalar.activation(rows[:, j % 2, a:b], picked(j, PAIRED + a, PAIRED + b), ACT.Copy)

        def fill_slots(copy, u, a, b):
            rows = (flat01, flat23)[u]
            copy(slotted[:, a:b, 2 * u : 2 * u + 2], rows[:, :, a:b].rearrange("p j s -> p s j"))

        def weave(copy, word, a, b):
            words = pairs.rearrange("p u s e -> p u (s e)").bitcast(word)[:, :, a:b]
            dst = woven[:, a * PACK : b * PACK].bitcast(word)
            copy(dst.rearrange("p (s u) -> p s u", u=2), words.rearrange("p u s -> p s u"))

        for j in range(PACK - 1):
            pair_gather(j, 0, PAIRED)
        nc.vector.tensor_copy(flat23[:, 0, 0:BY_VECTOR], picked(2, PAIRED, PAIRED + BY_VECTOR))
        for i in range(2):
            for j in range(2):
                flat_gather(j, i * P, (i + 1) * P)
        for i in range(2):
            fill_slots(nc.scalar.copy, 0, i * P, (i + 1) * P)
        flat_gather(2, BY_VECTOR, PAIRED)

        for i in range(2):
            pair_gather(3, i * P, (i + 1) * P)
        for i in range(2):
            flat_gather(3, i * P, (i + 1) * P)
        for i in range(2):
            fill_slots(nc.vector.tensor_copy, 1, i * P, (i + 1) * P)
        for i in range(2):
            weave(nc.scalar.copy, U32, i * P, (i + 1) * P)
        fused_shares = placed.tile([P, FUSED + V], F32, name="fused_shares", offset=STAGED_AT, align_bytes=64)
        nc.scalar.copy(fused_shares[:], spread[0][:].rearrange("p d v -> p (d v)")[:, V - FUSED : 2 * V])

        x_scales = keep.tile([P, S], U8, name="x_scales", align_bytes=64)
        y = keep.tile([P, S], F32, name="y")
        codes = {a: keep.tile([P, P], U32, name="codes%d" % a, align_bytes=64) for a in (0, P, PAIRED + P)}
        codes[PAIRED] = placed.tile([P, P], U32, name="codes%d" % PAIRED, offset=LAST_PLANE_AT, align_bytes=64)
        order = (PAIRED, 0, PAIRED + P, P)
        interleaved = {a: woven[:, a * PACK : (a + P) * PACK] for a in (0, P)}
        for i in range(2):
            interleaved[PAIRED + i * P] = slotted[:, i * P : (i + 1) * P, :].rearrange("p s j -> p (s j)")
        for a in order:
            nc.vector.quantize_mx(out=codes[a][:].bitcast(FP8X4), scales=x_scales[:, a : a + P], in_=interleaved[a])
        for a in order:
            acc = psum.tile([P, P], F32, name="acc%d" % a)
            nc.tensor.matmul_mx(
                out=acc[:],
                lhsT=w_codes[:].bitcast(FP8X4),
                lhsT_scale=w_scales[:],
                rhs=codes[a][:].bitcast(FP8X4),
                rhs_scale=x_scales[:, a : a + P],
                start=True,
                stop=True,
            )
            if a == order[-1]:
                nc.vector.tensor_copy(y[:, a : a + P], acc[:])
            else:
                nc.scalar.copy(y[:, a : a + P], acc[:])

        def neighbour(d, a, b):
            return y[:].indirect(places[d][:, a // PER_COLUMN : b // PER_COLUMN])

        cut = V - FUSED
        fetched = {d: keep.tile([P, V], F32, name="fetched%d" % d) for d in range(1, D)}
        terms = [keep.tile([P, V], F32, name="terms%d" % d) for d in range(D)]
        partial = keep.tile([P, V], F32, name="partial")
        result = keep.tile([P, V], F32, name="result")
        for d, a, b in ((1, 0, V), (3, 0, cut), (2, 0, P), (2, P, V)):
            nc.scalar.activation(fetched[d][:, a:b], neighbour(d, a, b), ACT.Copy)
        nc.vector.tensor_tensor(terms[0][:], neighbour(0, 0, V), fused_shares[:, FUSED:], ALU.mult)
        nc.vector.tensor_tensor(terms[3][:, cut:V], neighbour(3, cut, V), fused_shares[:, 0:FUSED], ALU.mult)

        def weigh(d, a, b):
            nc.vector.tensor_tensor(terms[d][:, a:b], fetched[d][:, a:b], share_of(d, a, b), ALU.mult)

        def add(dst, src, d, a, b):
            nc.vector.tensor_tensor(dst[:, a:b], src[:, a:b], terms[d][:, a:b], ALU.add)

        weigh(1, 0, V)
        weigh(3, 0, cut)
        add(terms[0], terms[0], 3, cut, V)
        add(partial, terms[0], 1, 0, P)
        weigh(2, 0, P)
        add(partial, terms[0], 1, P, V)
        weigh(2, P, V)
        add(partial, partial, 3, 0, P)
        add(result, partial, 2, P, V)
        add(result, partial, 2, 0, P)
        nc.sync.dma_start(out=out[:, :], in_=result[:])
